import numpy as np
import ml_dtypes


def mxq(x, axis, fmt="e4m3"):
    dtype, down = {"e4m3": (ml_dtypes.float8_e4m3fn, 7), "e5m2": (ml_dtypes.float8_e5m2, 14)}[fmt]
    v = np.moveaxis(np.asarray(x, np.float32).astype(ml_dtypes.bfloat16).astype(np.float64), axis, -1)
    blocks = v.reshape(v.shape[:-1] + (-1, 32))
    amax = np.abs(blocks).max(-1, keepdims=True)
    byte = np.maximum(np.where(amax > 0, np.frexp(amax)[1] - 1 + 127, 0) - down, 1)
    scale = np.exp2(byte - 127.0)
    codes = (blocks / scale).astype(np.float32).astype(dtype).astype(np.float64)
    return np.moveaxis((codes * scale).reshape(v.shape), -1, axis)


WIDE = False


def mx_kscale(k):
    if not WIDE:
        return np.ones(k)
    levels = np.array([10, -10, 5, -5, 0])
    if k % 512:
        return np.exp2(np.random.permutation(np.resize(levels, k // 32))).repeat(32)
    a = np.empty((k // 512, 16))
    for p in range(k // 512):
        a[p, :8] = np.random.permutation(np.resize(levels, 8))
        for g in range(8):
            far = levels[np.abs(levels - a[p, g]) >= 10]
            a[p, g + 8] = far[np.random.randint(len(far))]
    return np.exp2(a.ravel()).repeat(32)


BF16 = ml_dtypes.bfloat16


def bf(x):
    return np.asarray(x, np.float32).astype(BF16)


def f64(x):
    return np.asarray(x).astype(np.float64)


E2M1 = np.array([0.0, 0.5, 1.0, 1.5, 2.0, 3.0, 4.0, 6.0, -0.0, -0.5, -1.0, -1.5, -2.0, -3.0, -4.0, -6.0])


def pack_weight(w, fmt):
    k, n = w.shape
    w = f64(bf(w)).reshape(k // 32, 32, n)
    amax = np.abs(w).max(1)
    if fmt == "e4m3":
        byte = np.frexp(amax)[1] - 1 + 127 - 7
    else:
        mant, ex = np.frexp(amax / 6.0)
        byte = np.where(mant > 0.5, ex, ex - 1) + 127
    byte = np.clip(np.where(amax > 0, byte, 1), 1, 254)
    scaled = (w * np.exp2(127.0 - byte)[:, None, :]).reshape(k, n).astype(np.float32)
    by_word = np.ascontiguousarray(scaled.reshape(k // 512, 128, 4, n).transpose(0, 1, 3, 2))
    if fmt == "e4m3":
        words = by_word.astype(ml_dtypes.float8_e4m3fn).view(np.uint8)
    else:
        c = by_word.astype(ml_dtypes.float4_e2m1fn).view(np.uint8) & 0xF
        words = c[..., 0::2] | (c[..., 1::2] << 4)
    return np.ascontiguousarray(words), np.ascontiguousarray(byte.astype(np.uint8).reshape(k // 512, 16, n))


def unpack_weight(words, scales, fmt):
    g, p, n, _ = words.shape
    if fmt == "e4m3":
        vals = np.ascontiguousarray(words).view(ml_dtypes.float8_e4m3fn).astype(np.float64)
    else:
        nib = np.empty((g, p, n, 4), np.uint8)
        nib[..., 0::2] = words & 0xF
        nib[..., 1::2] = words >> 4
        vals = E2M1[nib]
    vals = vals * np.repeat(np.exp2(scales.astype(np.float64) - 127.0), 8, axis=1)[..., None]
    return vals.transpose(0, 1, 3, 2).reshape(g * 512, n)
def pack4(w):
    words, scales = pack_weight(w, "e2m1")
    return words.reshape(words.shape[0], 128, -1), scales


def unpack4(words, scales):
    return unpack_weight(words.reshape(words.shape[0], 128, -1, 2), scales, "e2m1")


E4M3FN = np.array([(-1.0 if i & 128 else 1.0) * ((1.0 + (i & 7) / 8.0) * 2.0 ** (((i >> 3) & 15) - 7) if i & 120 else (i & 7) * 2.0 ** -9) for i in range(256)])


def e4m3fn_bytes(y):
    return np.clip(np.asarray(y, np.float64), -448.0, 448.0).astype(np.float32).astype(ml_dtypes.float8_e4m3fn).view(np.uint8)


def e4m3fn_values(b):
    return E4M3FN[b]


P, N, T = 1024, 1024, 1024

CONC = 0.25


def draw0():
    s, t = mx_kscale(N), mx_kscale(N)
    signals = np.random.standard_normal((P, N)) * s
    u = np.random.standard_normal((N, N)) / np.sqrt(N) / s[:, None] * t
    u_words, u_scales = pack4(u)
    lam = np.random.uniform(0.7, 1.3, N)
    tilt = 1.0 + 0.1 * np.random.standard_normal(N)
    q = np.random.standard_normal((T, N)) / np.sqrt(N) / t
    return {"signals": bf(signals), "u_words": u_words, "u_scales": u_scales, "lam": bf(lam), "tilt": bf(tilt), "q": bf(q)}


def qis_eigenvalues(lam):
    n = lam.shape[0]
    c = CONC
    h = (c ** 2) ** 0.35 * float(n) ** (-0.35)
    l = 1.0 / lam
    l_j = l[:, None]
    d = l_j - l[None, :]
    den = d ** 2 + h ** 2 * l_j ** 2
    theta = np.mean(l_j * d / den, axis=0)
    eta = np.mean(h * l_j ** 2 / den, axis=0)
    amp2 = theta ** 2 + eta ** 2
    r = 1.0 / (l * ((1.0 - c) ** 2 + 2.0 * c * (1.0 - c) * theta + c ** 2 * amp2))
    return r * np.sum(lam) / np.sum(r)


def core(signals, u_words, u_scales, lam, tilt, q):
    delta = qis_eigenvalues(f64(lam))
    y = mxq(f64(signals), 1, "e4m3") @ unpack4(u_words, u_scales)
    x = y * f64(tilt)[None, :] / delta[None, :]
    return mxq(x, 1, "e4m3") @ mxq(f64(q), 1, "e4m3").T


def setup_inputs():
    drawn = draw0()
    full = np.asarray(drawn['signals']).astype(np.float64)
    scale = (np.abs(full).reshape(8, 128, 8, 128).max(axis=(1, 3)) / 448.0).astype(np.float32)
    given = {}
    for key, value in drawn.items():
        if key == 'signals':
            given['signals_bytes'] = e4m3fn_bytes(full / np.repeat(np.repeat(scale.astype(np.float64), 128, axis=0), 128, axis=1))
            given['signals_scale'] = scale
        else:
            given[key] = value
    return given


def reference(signals_bytes, signals_scale, u_words, u_scales, lam, tilt, q):
    return core(e4m3fn_values(signals_bytes) * np.repeat(np.repeat(signals_scale.astype(np.float64), 128, axis=0), 128, axis=1), u_words, u_scales, lam, tilt, q)

@@ -1,0 +1,363 @@
+from contextlib import ExitStack
+
+import concourse.mybir as mybir
+from concourse.masks import make_identity
+
+F32 = mybir.dt.float32
+BF16 = mybir.dt.bfloat16
+U8 = mybir.dt.uint8
+U32 = mybir.dt.uint32
+I32 = mybir.dt.int32
+FP8 = mybir.dt.float8_e4m3fn
+FP8X4 = mybir.dt.float8_e4m3fn_x4
+FP4X4 = mybir.dt.float4_e2m1fn_x4
+ALU = mybir.AluOpType
+ACT = mybir.ActivationFunctionType
+AXIS = mybir.AxisListType
+
+N = 1024
+P = 128
+HALF = 512
+TILES = N // P
+CONC = 0.25
+H = (CONC**2) ** 0.35 * float(N) ** (-0.35)
+FLOPS = 2 * 2 * N * N * N
+
+ORDER = """
+widen,0,0,S widen,1,0,V widen,0,1,S widen,1,1,S widen,2,0,V widen,3,0,V widen,2,1,V widen,3,1,V widen,4,0,V
+feat,0,0 feat,1,1 feato,0,S widen,5,0,V total,0,2 widen,4,1,V widen,5,1,V pw,1,V feato,1,S dist,0,0,3 root,0,0
+dist,0,1,4 dist,1,0,5 turn,0,0,6 pw,0,V root,0,1 root,1,0 dist,1,1,7 dist,2,0,0 dist,2,1,1 root,1,1 dist,3,0,3
+widen,6,0,V spread,4 root,2,0 eta,0,V dist,3,1,5 turn,0,1,7 root,2,1 turno,0,0,S psc,0,V eta,1,S dist,4,0,0
+dist,4,1,1 dist,5,0,6 turno,0,1,V root,3,0 eta,2,V turn,1,0,7 turn,1,1,3 theta,0 theta,1 root,3,1 root,4,0
+root,4,1 root,5,0 dist,5,1,5 dist,6,0,0 dist,6,1,1 turno,1,0,S widen,7,0,V quant,0,0 eta,3,S dist,7,0,6
+turno,1,1,V turn,2,0,7 turn,2,1,3 psc,1,V eta,4,S quant,0,1 root,5,1 root,6,0 s1,0,0,5 turn,3,0,0 eta,5,S
+widen,6,1,V theta,2 theta,3 theta,4 turno,2,0,S root,6,1 widen,7,1,S dist,7,1,7 root,7,0 eta,6,V turno,2,1,S
+turn,3,1,1 turn,4,0,6 turn,4,1,3 fin,0 root,7,1 s1,0,1,2 turno,3,0,S turno,3,1,S s1,0,2,7 eta,7,S turn,5,0,0
+theta,5 theta,6 quant,1,0 theta,7 turn,5,1,1 turno,4,0,S turno,4,1,S turno,5,0,S fin,3 fin,1 turno,5,1,S
+turn,6,0,6 turn,6,1,3 turn,7,0,4 fin,5 fin,4 fin,2 turno,6,0,S turn,7,1,0 fin,6 fin,7 fin,9 s1,0,3,1
+turno,6,1,S fin,8 fin,10 quant,2,1 turno,7,0,S total,1,6 s1,0,4,3 turno,7,1,S fin,11 quant,1,1 s1,0,5,4
+yo,0,0,S quant,3,0 s1,0,6,6 yo,0,1,V yo,0,2,S s1,0,7,0 s1,1,0,5 yo,0,3,S yo,0,4,S s1,1,1,7 yo,0,5,S yo,0,6,V
+yo,0,7,V quant,2,0 s1,1,2,2 il,0,0,S il,0,1,V s1,1,3,1 quant,3,1 yo,1,0,S s1,1,4,6 il,1,0,V yo,1,1,V yo,1,2,S
+s1,1,5,3 yo,1,3,S qx,0,0 s1,1,6,0 il,1,1,V yo,1,4,S s1,1,7,4 il,2,0,V qx,0,1 il,2,1,V yo,1,5,S qx,1,0 s2,0,0,5
+il,3,1,V yo,1,6,S qx,1,1 qx,2,0 s2,0,1,2 res,0,0,S s2,1,1,7 yo,1,7,V il,3,0,V res,0,1,S s2,1,0,1 qx,2,1
+il,4,1,V res,1,1,S s2,2,1,6 qx,3,1 il,4,0,V res,1,0,S s2,2,0,3 qx,3,0 il,5,1,V res,2,1,S qx,4,0 s2,3,0,0
+qx,4,1 il,6,1,V res,2,0,S s2,4,0,4 il,7,1,V qx,5,1 res,3,0,S s2,3,1,5 qx,6,1 il,5,0,V il,6,0,V s2,4,1,2
+res,4,0,S qx,5,0 res,3,1,S qx,6,0 res,4,1,V qx,7,1 il,7,0,S s2,5,0,7 res,5,0,V s2,6,0,1 res,6,0,V s2,5,1,6
+res,5,1,S s2,6,1,3 res,6,1,S qx,7,0 s2,7,0,0 res,7,0,V s2,7,1,4 res,7,1,S
+"""
+
+
+def tile_quadraticinverseshrinkagesignalpnl_d2p_kernel(
+    tc, signals_bytes, signals_scale, u_words, u_scales, lam, tilt, q, out
+):
+    nc = tc.nc
+    with ExitStack() as ctx:
+        keep = ctx.enter_context(tc.tile_pool(name="keep", bufs=1))
+        psum = ctx.enter_context(tc.psum_pool(name="psum", bufs=1))
+        ctx.enter_context(tc.manual_schedule())
+
+        def sb(name, shape, dtype):
+            return keep.tile(shape, dtype, name=name, align_bytes=64)
+
+        def small(name, width=TILES):
+            return sb(name, [P, width], F32)
+
+        def bank(index, name, shape, dtype):
+            return psum.tile(shape, dtype, name=name, tag="bank%d" % index)
+
+        def copy(engine, dst, src):
+            if engine == "S":
+                nc.scalar.copy(out=dst, in_=src)
+            elif engine == "G":
+                nc.gpsimd.tensor_copy(out=dst, in_=src)
+            else:
+                nc.vector.tensor_copy(out=dst, in_=src)
+
+        def scaled(engine, dst, src, factor):
+            if engine == "S":
+                nc.scalar.activation(out=dst, in_=src, func=ACT.Copy, scale=factor)
+            else:
+                nc.vector.tensor_scalar(out=dst, in0=src, scalar1=factor, scalar2=None, op0=ALU.mult)
+
+        ident16 = sb("ident16", [P, P], BF16)
+        ident32 = sb("ident32", [P, P], F32)
+        ones32 = sb("ones32", [P, P], F32)
+        warm = sb("warm", [P, 8], F32)
+        lam16 = sb("lam16", [P, 2, 4], BF16)
+        tilt16 = sb("tilt16", [P, 2, 4], BF16)
+        block_scale = sb("block_scale", [P, TILES * TILES], F32)
+        sig_bytes = [sb("sig_bytes%d" % j, [P, 2, N], U8) for j in range(4)]
+        q_rows = [sb("q_rows%d" % j, [P, 2, N], BF16) for j in range(4)]
+        u_words_raw = sb("u_words_raw", [P, 2, 2 * N], U8)
+        u_scales_raw = sb("u_scales_raw", [P, 2, N], U8)
+        u_w = sb("u_w", [P, 2, 2 * N], U8)
+        u_s = sb("u_s", [P, 2, N], U8)
+        feat_i = sb("feat_i", [P, TILES, P], BF16)
+        feat_j = sb("feat_j", [P, TILES, P], BF16)
+        rows_i = sb("rows_i", [P, N], BF16)
+        rows_j = sb("rows_j", [P, N], BF16)
+        lam_flat = lam16[:].rearrange("p g t -> p (g t)")
+        tilt_flat = tilt16[:].rearrange("p g t -> p (g t)")
+
+        sig_view = signals_bytes.rearrange("(r p) k -> p r k", p=P)
+        q_view = q.rearrange("(r p) k -> p r k", p=P)
+        nc.sync.dma_start(out=lam16[:], in_=lam.rearrange("(g p t) -> p g t", p=P, t=4))
+        nc.sync.dma_start(out=block_scale[:], in_=signals_scale.rearrange("a b -> (a b)").partition_broadcast(P))
+        for j in range(4):
+            nc.sync.dma_start(out=sig_bytes[j][:], in_=sig_view[:, 2 * j : 2 * j + 2, :])
+        nc.vector.memset(warm[:], 1.0)
+        nc.vector.memset(u_scales_raw[:].bitcast(I32), 0)
+        nc.scalar.activation(out=warm[:, 0:1], in_=warm[:, 1:2], func=ACT.Abs_reciprocal_sqrt)
+        nc.sync.dma_start(out=tilt16[:], in_=tilt.rearrange("(g p t) -> p g t", p=P, t=4))
+        for quad in range(4):
+            nc.sync.dma_start(
+                out=u_scales_raw[32 * quad : 32 * quad + 4].bitcast(I32),
+                in_=u_scales[:, 4 * quad : 4 * quad + 4, :].rearrange("g r n -> r g n").bitcast(I32),
+            )
+        nc.sync.dma_start(out=u_words_raw[:].bitcast(I32), in_=u_words.rearrange("g p n -> p g n").bitcast(I32))
+        for j in range(4):
+            nc.sync.dma_start(out=q_rows[j][:], in_=q_view[:, 2 * j : 2 * j + 2, :])
+
+        make_identity(nc, ident16[:])
+        make_identity(nc, ident32[:])
+        nc.vector.memset(feat_j[:], 0.0)
+        nc.vector.memset(feat_i[:], 0.0)
+        nc.vector.memset(feat_j[:, :, 1:3], 1.0)
+        nc.vector.memset(feat_i[:, :, 3:5], 1.0)
+        nc.vector.memset(ones32[:], 1.0)
+
+        lam_sq = small("lam_sq")
+        nc.vector.tensor_tensor(out=lam_sq[:], in0=lam_flat, in1=lam_flat, op=ALU.mult)
+        nc.vector.tensor_scalar(out=feat_j[:, :, 0], in0=lam_flat, scalar1=-2.0, scalar2=None, op0=ALU.mult)
+        nc.vector.tensor_copy(out=feat_i[:, :, 0], in_=lam_flat)
+        nc.vector.tensor_copy(out=feat_j[:, :, 3], in_=lam_sq[:])
+        nc.vector.tensor_copy(out=feat_i[:, :, 1], in_=lam_sq[:])
+        nc.vector.tensor_tensor(out=feat_j[:, :, 4], in0=lam_sq[:], in1=feat_j[:, :, 3], op=ALU.subtract)
+        nc.vector.tensor_tensor(out=feat_i[:, :, 2], in0=lam_sq[:], in1=feat_i[:, :, 1], op=ALU.subtract)
+
+        ridge = small("ridge")
+        eta_root = small("eta_root")
+        eta_coef = small("eta_coef")
+        two_a = small("two_a")
+        theta_shift = small("theta_shift")
+        two_ha = small("two_ha")
+        cube = small("cube")
+        lam_part = small("lam_part", 1)
+        root = (CONC * H / N) ** 0.5
+        nc.scalar.activation(out=ridge[:], in_=lam_flat, func=ACT.Square, scale=H)
+        nc.scalar.activation(out=eta_root[:], in_=lam_flat, func=ACT.Copy, scale=root)
+        nc.scalar.activation(out=eta_coef[:], in_=lam_flat, func=ACT.Square, scale=root)
+        nc.scalar.activation(out=two_a[:], in_=lam_flat, func=ACT.Copy, scale=2.0)
+        nc.scalar.activation(out=theta_shift[:], in_=lam_flat, func=ACT.Copy, scale=2.0 * H * (1.0 - CONC))
+        nc.scalar.activation(out=two_ha[:], in_=lam_flat, func=ACT.Copy, scale=2.0 * H)
+        nc.vector.tensor_reduce(out=lam_part[:], in_=lam_flat, axis=AXIS.X, op=ALU.add)
+        nc.vector.scalar_tensor_tensor(out=cube[:], in0=ridge[:], scalar=4.0, in1=lam_flat, op0=ALU.mult, op1=ALU.mult)
+
+        sig_wide = [sb("sig_wide%d" % r, [P, N], BF16) for r in range(TILES)]
+        sig_t = [sb("sig_t%d" % h, [P, 2, HALF, 4], BF16) for h in range(2)]
+        q_t = [sb("q_t%d" % h, [P, 2, HALF, 4], BF16) for h in range(2)]
+        x_t = [sb("x_t%d" % h, [P, 2, HALF, 4], BF16) for h in range(2)]
+        x_planes = [sb("x_planes%d" % h, [P, 2, 4, HALF], BF16) for h in range(2)]
+        codes = [sb("codes%d" % h, [P, 2, HALF], U32) for h in range(6)]
+        scales = [sb("scales%d" % h, [P, 2, HALF], U8) for h in range(6)]
+        grouped = sig_t + q_t + x_t
+        result = [sb("result%d" % r, [P, N], F32) for r in range(TILES)]
+        kern = [sb("kern%d" % c, [P, N], F32) for c in range(TILES)]
+        eta_sum = small("eta_sum")
+        theta_sum = small("theta_sum")
+        tilt_coef = small("tilt_coef")
+        eta_sq = small("eta_sq")
+        shifted = small("shifted")
+        energy = small("energy")
+        inv_energy = small("inv_energy")
+        r_values = small("r_values")
+        r_part = small("r_part", 1)
+        tilted = small("tilted")
+        factor = small("factor")
+        ps = {}
+
+        def features(side, index):
+            ps["feat", side] = bank(index, "feat_ps%d" % side, [P, N], BF16)
+            for c in range(TILES):
+                nc.tensor.matmul(
+                    ps["feat", side][:, c * P : (c + 1) * P], lhsT=(feat_j, feat_i)[side][:, c, :], rhs=ident16[:],
+                    start=True, stop=True,
+                )
+
+        def features_out(side, engine):
+            copy(engine, (rows_j, rows_i)[side][:], ps["feat", side][:])
+
+        def total(which, index):
+            ps["total", which] = bank(index, "total%d" % which, [P, 1], F32)
+            nc.tensor.matmul(ps["total", which][:], lhsT=ones32[:], rhs=(lam_part, r_part)[which][:], start=True, stop=True)
+
+        def spread(index):
+            ps["spread"] = bank(index, "minus_2b", [P, N], BF16)
+            for h in range(2):
+                nc.tensor.matmul(
+                    ps["spread"][:, h * HALF : (h + 1) * HALF], lhsT=ident16[:, 0:1].to_broadcast([P, P]),
+                    rhs=rows_j[:, h * HALF : (h + 1) * HALF], start=True, stop=True,
+                )
+
+        def widen(r, g, engine):
+            for b in range(4 * g, 4 * g + 4):
+                cols = slice(b * P, (b + 1) * P)
+                scaled(
+                    engine, sig_wide[r][:, cols], sig_bytes[r // 2][:, r % 2, cols].bitcast(FP8),
+                    block_scale[:, r * TILES + b : r * TILES + b + 1],
+                )
+
+        def turn(pair, g, index):
+            ps["turn", pair, g] = bank(index, "turn%d_%d" % (pair, g), [P, 2, 2, P], F32)
+            for a in range(2):
+                rows = sig_wide[2 * pair + a][:] if pair < 4 else q_rows[pair - 4][:, a, :]
+                words = rows.bitcast(F32)
+                for u in range(2):
+                    nc.tensor.transpose(ps["turn", pair, g][:, a, u, :], words[:, 256 * g + u : 256 * (g + 1) : 2], ident32[:])
+
+        def turn_out(pair, g, engine):
+            dst = grouped[pair // 2][:, g, (pair % 2) * 2 * P : (pair % 2 + 1) * 2 * P, :].bitcast(F32)
+            copy(engine, dst.rearrange("p (a r) u -> p a r u", a=2), ps["turn", pair, g][:].rearrange("p a u r -> p a r u"))
+
+        def quantise(k, g):
+            nc.vector.quantize_mx(
+                out=codes[k][:, g, :].bitcast(FP8X4), scales=scales[k][:, g, :],
+                in_=grouped[k][:, g].rearrange("p c t -> p (c t)"),
+            )
+
+        def permute_words(g, engine):
+            copy(
+                engine,
+                u_w[:, g, :].rearrange("p (h t m b) -> p h t m b", h=2, t=4, b=2),
+                u_words_raw[:, g, :].rearrange("p (h m t b) -> p h t m b", h=2, t=4, b=2),
+            )
+
+        def permute_scales(g, engine):
+            copy(
+                engine,
+                u_s[:, g, :].rearrange("p (h t m) -> p h t m", h=2, t=4),
+                u_scales_raw[:, g, :].rearrange("p (h m t) -> p h t m", h=2, t=4),
+            )
+
+        def distance(c, h, index):
+            ps["dist", c, h] = bank(index, "dist%d_%d" % (c, h), [P, HALF], F32)
+            nc.tensor.matmul(
+                ps["dist", c, h][:], lhsT=rows_i[:, c * P : (c + 1) * P], rhs=rows_j[:, h * HALF : (h + 1) * HALF],
+                start=True, stop=True,
+            )
+
+        def inv_root(c, h):
+            nc.scalar.activation(
+                out=kern[c][:, h * HALF : (h + 1) * HALF], in_=ps["dist", c, h][:], func=ACT.Abs_reciprocal_sqrt,
+                bias=ridge[:, c : c + 1],
+            )
+
+        def eta_pass(c, engine):
+            if engine == "S":
+                nc.scalar.activation(
+                    out=kern[c][:], in_=kern[c][:], func=ACT.Square, scale=eta_root[:, c : c + 1],
+                    accum_out=eta_sum[:, c : c + 1],
+                )
+            else:
+                nc.vector.scalar_tensor_tensor(
+                    out=kern[c][:], in0=kern[c][:], scalar=eta_coef[:, c : c + 1], in1=kern[c][:],
+                    op0=ALU.mult, op1=ALU.mult, accum_out=eta_sum[:, c : c + 1],
+                )
+
+        def theta_pass(c):
+            nc.vector.scalar_tensor_tensor(
+                out=kern[c][:], in0=ps["spread"][:], scalar=two_a[:, c : c + 1], in1=kern[c][:],
+                op0=ALU.add, op1=ALU.mult, accum_out=theta_sum[:, c : c + 1],
+            )
+
+        def product(dst, a, b, op):
+            nc.vector.tensor_tensor(out=dst[:], in0=a, in1=b, op=op)
+
+        def finish(k):
+            if k == 0:
+                scaled("V", tilt_coef[:], cube[:], ps["total", 0][:, 0:1])
+            if k == 1:
+                nc.vector.reciprocal(out=tilt_coef[:], in_=tilt_coef[:])
+            if k == 2:
+                product(tilt_coef, tilt_coef[:], tilt_flat, ALU.mult)
+            if k == 3:
+                product(eta_sq, eta_sum[:], two_ha[:], ALU.mult)
+            if k == 4:
+                product(eta_sq, eta_sq[:], eta_sq[:], ALU.mult)
+            if k == 5:
+                product(shifted, theta_sum[:], theta_shift[:], ALU.add)
+            if k == 6:
+                product(shifted, shifted[:], shifted[:], ALU.mult)
+            if k == 7:
+                product(energy, shifted[:], eta_sq[:], ALU.add)
+            if k == 8:
+                nc.vector.reciprocal(out=inv_energy[:], in_=energy[:])
+            if k == 9:
+                product(tilted, energy[:], tilt_coef[:], ALU.mult)
+            if k == 10:
+                nc.vector.scalar_tensor_tensor(
+                    out=r_values[:], in0=inv_energy[:], scalar=1.0, in1=cube[:], op0=ALU.mult, op1=ALU.mult,
+                    accum_out=r_part[:],
+                )
+            if k == 11:
+                scaled("V", factor[:], tilted[:], ps["total", 1][:, 0:1])
+
+        def stage1(h, c, index):
+            ps["y", h, c] = bank(index, "y%d_%d" % (h, c), [P, HALF], F32)
+            for g in range(2):
+                nc.tensor.matmul_mx(
+                    out=ps["y", h, c][:],
+                    lhsT=u_w[:, g, 2 * P * c : 2 * P * (c + 1)].bitcast(FP4X4),
+                    lhsT_scale=u_s[:, g, P * c : P * (c + 1)],
+                    rhs=codes[h][:, g, :].bitcast(FP8X4),
+                    rhs_scale=scales[h][:, g, :],
+                    start=(g == 0),
+                    stop=(g == 1),
+                )
+
+        def y_out(h, c, engine):
+            scaled(engine, x_planes[h][:, c // 4, c % 4, :], ps["y", h, c][:], factor[:, c : c + 1])
+
+        def interleave(r, g, engine):
+            cols = slice((r % 4) * P, (r % 4 + 1) * P)
+            copy(
+                engine,
+                x_t[r // 4][:, g, cols, :].rearrange("p (c i) t -> p c t i", i=4),
+                x_planes[r // 4][:, g, :, cols].rearrange("p t (c i) -> p c t i", i=4),
+            )
+
+        def quantise_x(r, g):
+            cols = slice((r % 4) * P, (r % 4 + 1) * P)
+            nc.vector.quantize_mx(
+                out=codes[4 + r // 4][:, g, cols].bitcast(FP8X4), scales=scales[4 + r // 4][:, g, cols],
+                in_=x_t[r // 4][:, g, cols, :].rearrange("p c t -> p (c t)"),
+            )
+
+        def stage2(r, th, index):
+            ps["out", r, th] = bank(index, "o%d_%d" % (r, th), [P, HALF], F32)
+            cols = slice((r % 4) * P, (r % 4 + 1) * P)
+            for g in range(2):
+                nc.tensor.matmul_mx(
+                    out=ps["out", r, th][:],
+                    lhsT=codes[4 + r // 4][:, g, cols].bitcast(FP8X4),
+                    lhsT_scale=scales[4 + r // 4][:, g, cols],
+                    rhs=codes[2 + th][:, g, :].bitcast(FP8X4),
+                    rhs_scale=scales[2 + th][:, g, :],
+                    start=(g == 0),
+                    stop=(g == 1),
+                )
+
+        def result_out(r, th, engine):
+            cols = slice(th * HALF, (th + 1) * HALF)
+            copy(engine, result[r][:, cols], ps["out", r, th][:])
+            nc.sync.dma_start(out=out[r * P : (r + 1) * P, cols], in_=result[r][:, cols])
+
+        steps = {
+            "feat": features, "feato": features_out, "total": total, "spread": spread, "widen": widen, "turn": turn,
+            "turno": turn_out, "quant": quantise, "pw": permute_words, "psc": permute_scales, "dist": distance,
+            "root": inv_root, "eta": eta_pass, "theta": theta_pass, "fin": finish, "s1": stage1, "yo": y_out,
+            "il": interleave, "qx": quantise_x, "s2": stage2, "res": result_out,
+        }
+        for word in ORDER.split():
+            parts = word.split(",")
+            steps[parts[0]](*[(x if x in "SVG" else int(x)) for x in parts[1:]])

@@ -24,26 +24,23 @@ H = (CONC**2) ** 0.35 * float(N) ** (-0.35)
 FLOPS = 2 * 2 * N * N * N
 
 ORDER = """
-widen,0,0,S widen,1,0,V widen,0,1,S widen,1,1,S widen,2,0,V widen,3,0,V widen,2,1,V widen,3,1,V widen,4,0,V
-feat,0,0 feat,1,1 feato,0,S widen,5,0,V total,0,2 widen,4,1,V widen,5,1,V pw,1,V feato,1,S dist,0,0,3 root,0,0
-dist,0,1,4 dist,1,0,5 turn,0,0,6 pw,0,V root,0,1 root,1,0 dist,1,1,7 dist,2,0,0 dist,2,1,1 root,1,1 dist,3,0,3
-widen,6,0,V spread,4 root,2,0 eta,0,V dist,3,1,5 turn,0,1,7 root,2,1 turno,0,0,S psc,0,V eta,1,S dist,4,0,0
-dist,4,1,1 dist,5,0,6 turno,0,1,V root,3,0 eta,2,V turn,1,0,7 turn,1,1,3 theta,0 theta,1 root,3,1 root,4,0
-root,4,1 root,5,0 dist,5,1,5 dist,6,0,0 dist,6,1,1 turno,1,0,S widen,7,0,V quant,0,0 eta,3,S dist,7,0,6
-turno,1,1,V turn,2,0,7 turn,2,1,3 psc,1,V eta,4,S quant,0,1 root,5,1 root,6,0 s1,0,0,5 turn,3,0,0 eta,5,S
-widen,6,1,V theta,2 theta,3 theta,4 turno,2,0,S root,6,1 widen,7,1,S dist,7,1,7 root,7,0 eta,6,V turno,2,1,S
-turn,3,1,1 turn,4,0,6 turn,4,1,3 fin,0 root,7,1 s1,0,1,2 turno,3,0,S turno,3,1,S s1,0,2,7 eta,7,S turn,5,0,0
-theta,5 theta,6 quant,1,0 theta,7 turn,5,1,1 turno,4,0,S turno,4,1,S turno,5,0,S fin,3 fin,1 turno,5,1,S
-turn,6,0,6 turn,6,1,3 turn,7,0,4 fin,5 fin,4 fin,2 turno,6,0,S turn,7,1,0 fin,6 fin,7 fin,9 s1,0,3,1
-turno,6,1,S fin,8 fin,10 quant,2,1 turno,7,0,S total,1,6 s1,0,4,3 turno,7,1,S fin,11 quant,1,1 s1,0,5,4
-yo,0,0,S quant,3,0 s1,0,6,6 yo,0,1,V yo,0,2,S s1,0,7,0 s1,1,0,5 yo,0,3,S yo,0,4,S s1,1,1,7 yo,0,5,S yo,0,6,V
-yo,0,7,V quant,2,0 s1,1,2,2 il,0,0,S il,0,1,V s1,1,3,1 quant,3,1 yo,1,0,S s1,1,4,6 il,1,0,V yo,1,1,V yo,1,2,S
-s1,1,5,3 yo,1,3,S qx,0,0 s1,1,6,0 il,1,1,V yo,1,4,S s1,1,7,4 il,2,0,V qx,0,1 il,2,1,V yo,1,5,S qx,1,0 s2,0,0,5
-il,3,1,V yo,1,6,S qx,1,1 qx,2,0 s2,0,1,2 res,0,0,S s2,1,1,7 yo,1,7,V il,3,0,V res,0,1,S s2,1,0,1 qx,2,1
-il,4,1,V res,1,1,S s2,2,1,6 qx,3,1 il,4,0,V res,1,0,S s2,2,0,3 qx,3,0 il,5,1,V res,2,1,S qx,4,0 s2,3,0,0
-qx,4,1 il,6,1,V res,2,0,S s2,4,0,4 il,7,1,V qx,5,1 res,3,0,S s2,3,1,5 qx,6,1 il,5,0,V il,6,0,V s2,4,1,2
-res,4,0,S qx,5,0 res,3,1,S qx,6,0 res,4,1,V qx,7,1 il,7,0,S s2,5,0,7 res,5,0,V s2,6,0,1 res,6,0,V s2,5,1,6
-res,5,1,S s2,6,1,3 res,6,1,S qx,7,0 s2,7,0,0 res,7,0,V s2,7,1,4 res,7,1,S
+widen,0,S widen,1,V feat,0,0 feat,1,1 feato,1,S feat,2,2 widen,2,S widen,3,V widen,4,G ktab feat,3,3 feato,3,S
+feato,0,V feato,2,V dist,0,0,4 dist,0,1,5 psc,1,V root,0,0 turn,0,0,6 pw,1,V root,0,1 turn,0,1,7 spread,1
+eta,0,S sigo,0,0 widen,5,G dist,1,0,0 dist,1,1,2 sigo,0,1 turn,1,0,3 root,1,0 theta,0 dist,2,0,4 root,1,1
+widen,6,G turn,1,1,5 eta,1,S turn,2,0,6 sigo,1,0 dist,2,1,7 psc,0,G sigo,1,1 dist,3,0,0 root,2,0 turn,2,1,2
+sigo,2,0 root,2,1 dist,3,1,3 theta,1 root,3,0 widen,7,G dist,4,0,5 dist,4,1,4 root,3,1 dist,5,0,6 dist,5,1,7
+sigo,2,1 root,4,0 quant,0 turn,3,0,0 eta,2,S turn,3,1,3 sigo,3,0 rg,0,G root,4,1 theta,2 root,5,0 eta,3,V
+eta,4,S turn,4,0,2 root,5,1 dist,6,0,5 pw,0,G sigo,3,1 turno,4,0,S total,0,0 eta,5,S theta,3 dist,6,1,4
+dist,7,0,6 turn,4,1,7 theta,4 root,6,0 dist,7,1,2 root,6,1 quant,1 s1t,0,0,3 root,7,0 root,7,1 eta,6,S fin,0
+rg,1,V s1,1,0,5 s1t,0,1,4 rg,2,G theta,5 eta,7,S turn,5,0,6 s1t,1,0,2 theta,6 turno,4,1,S rg,3,G turn,5,1,0
+turno,5,0,S theta,7 turn,6,0,7 turno,5,1,S turn,6,1,6 turno,6,0,S fin,3 turn,7,0,0 fin,5 turno,6,1,S fin,1
+turn,7,1,1 fin,4 fin,6 fin,2 turno,7,0,S fin,7 s1t,1,1,7 fin,8 fin,9 turno,7,1,S fin,10 quant,2 s1,1,1,6
+total,1,0 s1t,2,0,1 fin,11 s1,1,2,0 yd,0,0 yo,1,0,S yo,1,1,S s1,1,3,5 yd,0,1 yo,1,2,S s1,1,4,3 yd,1,0 yo,1,3,S
+s1,1,5,6 quant,3 yo,1,4,S s1,1,6,4 s1,1,7,0 yo,1,5,S yo,1,6,V s1t,2,1,2 yo,1,7,S qx,0 yd,1,1 s1t,3,0,5 il,4,S
+il,5,G yd,2,0 s2,0,1,3 yd,2,1 s2,0,0,6 s1t,3,1,4 qx,1 res,0,0,S qx,2 s2,1,1,0 il,6,G yd,3,0 res,0,1,S s2,1,0,7
+yd,3,1 res,1,1,S s2,2,0,1 res,1,0,S s2,2,1,2 qx,3 res,2,0,V s2,3,1,6 res,2,1,S qx,4 s2,3,0,3 qx,5 res,3,1,S
+qx,6 s2,4,0,5 il,7,V s2,5,0,4 res,3,0,S res,4,0,S res,5,0,V s2,4,1,0 s2,5,1,7 res,4,1,S qx,7 s2,6,1,1
+res,5,1,S s2,7,1,2 res,6,1,V s2,6,0,6 res,7,1,S s2,7,0,3 res,6,0,S res,7,0,V
 """
 
 
@@ -156,11 +153,15 @@ def tile_quadraticinverseshrinkagesignalpnl_d2p_kernel(
         sig_wide = [sb("sig_wide%d" % r, [P, N], BF16) for r in range(TILES)]
         sig_t = [sb("sig_t%d" % h, [P, 2, HALF, 4], BF16) for h in range(2)]
         q_t = [sb("q_t%d" % h, [P, 2, HALF, 4], BF16) for h in range(2)]
-        x_t = [sb("x_t%d" % h, [P, 2, HALF, 4], BF16) for h in range(2)]
-        x_planes = [sb("x_planes%d" % h, [P, 2, 4, HALF], BF16) for h in range(2)]
-        codes = [sb("codes%d" % h, [P, 2, HALF], U32) for h in range(6)]
-        scales = [sb("scales%d" % h, [P, 2, HALF], U8) for h in range(6)]
-        grouped = sig_t + q_t + x_t
+        x_t = [sb("x_t%d" % r, [P, 2, P, 4], BF16) for r in range(TILES)]
+        x_planes = sb("x_planes", [P, 2, 4, HALF], BF16)
+        x_codes = [sb("x_codes%d" % r, [P, 2, P], U32) for r in range(TILES)]
+        x_scales = [sb("x_scales%d" % r, [P, 2, P], U8) for r in range(TILES)]
+        codes = [sb("codes%d" % h, [P, 2, HALF], U32) for h in range(4)]
+        scales = [sb("scales%d" % h, [P, 2, HALF], U8) for h in range(4)]
+        grouped = sig_t + q_t
+        q_split = [sb("q_split%d" % j, [P, 2, HALF], F32) for j in range(4)]
+        k_scale = sb("k_scale", [P, TILES, 2], F32)
         result = [sb("result%d" % r, [P, N], F32) for r in range(TILES)]
         kern = [sb("kern%d" % c, [P, N], F32) for c in range(TILES)]
         eta_sum = small("eta_sum")
@@ -176,16 +177,20 @@ def tile_quadraticinverseshrinkagesignalpnl_d2p_kernel(
         factor = small("factor")
         ps = {}
 
-        def features(side, index):
-            ps["feat", side] = bank(index, "feat_ps%d" % side, [P, N], BF16)
-            for c in range(TILES):
+        pieces = ((0, 0, 4), (1, 0, 2), (0, 4, 8), (1, 2, 8))
+
+        def features(k, index):
+            side, first, last = pieces[k]
+            ps["feat", k] = bank(index, "feat_ps%d" % k, [P, (last - first) * P], BF16)
+            for c in range(first, last):
                 nc.tensor.matmul(
-                    ps["feat", side][:, c * P : (c + 1) * P], lhsT=(feat_j, feat_i)[side][:, c, :], rhs=ident16[:],
-                    start=True, stop=True,
+                    ps["feat", k][:, (c - first) * P : (c - first + 1) * P], lhsT=(feat_j, feat_i)[side][:, c, :],
+                    rhs=ident16[:], start=True, stop=True,
                 )
 
-        def features_out(side, engine):
-            copy(engine, (rows_j, rows_i)[side][:], ps["feat", side][:])
+        def features_out(k, engine):
+            side, first, last = pieces[k]
+            copy(engine, (rows_j, rows_i)[side][:, first * P : last * P], ps["feat", k][:])
 
         def total(which, index):
             ps["total", which] = bank(index, "total%d" % which, [P, 1], F32)
@@ -199,30 +204,49 @@ def tile_quadraticinverseshrinkagesignalpnl_d2p_kernel(
                     rhs=rows_j[:, h * HALF : (h + 1) * HALF], start=True, stop=True,
                 )
 
-        def widen(r, g, engine):
-            for b in range(4 * g, 4 * g + 4):
-                cols = slice(b * P, (b + 1) * P)
-                scaled(
-                    engine, sig_wide[r][:, cols], sig_bytes[r // 2][:, r % 2, cols].bitcast(FP8),
-                    block_scale[:, r * TILES + b : r * TILES + b + 1],
+        def scale_table():
+            for quad in range(4):
+                rows = slice(32 * quad, 32 * quad + 32)
+                nc.vector.tensor_copy(
+                    out=k_scale[rows], in_=block_scale[rows].rearrange("p (r g b) -> p r g b", g=2, b=4)[:, :, :, quad]
                 )
+
+        def widen(r, engine):
+            copy(engine, sig_wide[r][:], sig_bytes[r // 2][:, r % 2, :].bitcast(FP8))
+
+        def regroup(pair, engine):
+            copy(
+                engine,
+                q_split[pair][:].rearrange("p a (g u m) -> p (a g) u m", g=2, u=2),
+                q_rows[pair][:].bitcast(F32).rearrange("p a (g m u) -> p (a g) u m", g=2, u=2),
+            )
 
         def turn(pair, g, index):
             ps["turn", pair, g] = bank(index, "turn%d_%d" % (pair, g), [P, 2, 2, P], F32)
             for a in range(2):
-                rows = sig_wide[2 * pair + a][:] if pair < 4 else q_rows[pair - 4][:, a, :]
-                words = rows.bitcast(F32)
                 for u in range(2):
-                    nc.tensor.transpose(ps["turn", pair, g][:, a, u, :], words[:, 256 * g + u : 256 * (g + 1) : 2], ident32[:])
+                    if pair < 4:
+                        words = sig_wide[2 * pair + a][:].bitcast(F32)[:, 256 * g + u : 256 * (g + 1) : 2]
+                    else:
+                        words = q_split[pair - 4][:, a, (2 * g + u) * P : (2 * g + u + 1) * P]
+                    nc.tensor.transpose(ps["turn", pair, g][:, a, u, :], words, ident32[:])
 
         def turn_out(pair, g, engine):
             dst = grouped[pair // 2][:, g, (pair % 2) * 2 * P : (pair % 2 + 1) * 2 * P, :].bitcast(F32)
             copy(engine, dst.rearrange("p (a r) u -> p a r u", a=2), ps["turn", pair, g][:].rearrange("p a u r -> p a r u"))
 
-        def quantise(k, g):
+        def signals_out(pair, g):
+            for a in range(2):
+                r = 2 * pair + a
+                dst = sig_t[r // 4][:, g, (r % 4) * P : (r % 4 + 1) * P, :].rearrange("p c (u e) -> p c u e", u=2)
+                src = ps["turn", pair, g][:, a].rearrange("p u c -> p (u c)").bitcast(BF16)
+                scaled("V", dst, src.rearrange("p (u c e) -> p c u e", u=2, e=2), k_scale[:, r, g : g + 1])
+
+        def quantise(k):
             nc.vector.quantize_mx(
-                out=codes[k][:, g, :].bitcast(FP8X4), scales=scales[k][:, g, :],
-                in_=grouped[k][:, g].rearrange("p c t -> p (c t)"),
+                out=codes[k][:].rearrange("p g c -> p (g c)").bitcast(FP8X4),
+                scales=scales[k][:].rearrange("p g c -> p (g c)"),
+                in_=grouped[k][:].rearrange("p g c t -> p (g c t)"),
             )
 
         def permute_words(g, engine):
@@ -315,32 +339,55 @@ def tile_quadraticinverseshrinkagesignalpnl_d2p_kernel(
                     stop=(g == 1),
                 )
 
-        def y_out(h, c, engine):
-            scaled(engine, x_planes[h][:, c // 4, c % 4, :], ps["y", h, c][:], factor[:, c : c + 1])
+        def stage1_tile(r, g2, index):
+            ps["yt", r, g2] = bank(index, "yt%d_%d" % (r, g2), [P, 4, P], F32)
+            cols = slice((r % 4) * P, (r % 4 + 1) * P)
+            for t in range(4):
+                c = 4 * g2 + t
+                for g in range(2):
+                    nc.tensor.matmul_mx(
+                        out=ps["yt", r, g2][:, t, :],
+                        lhsT=u_w[:, g, 2 * P * c : 2 * P * (c + 1)].bitcast(FP4X4),
+                        lhsT_scale=u_s[:, g, P * c : P * (c + 1)],
+                        rhs=codes[r // 4][:, g, cols].bitcast(FP8X4),
+                        rhs_scale=scales[r // 4][:, g, cols],
+                        start=(g == 0),
+                        stop=(g == 1),
+                    )
 
-        def interleave(r, g, engine):
+        def y_direct(r, g2):
+            nc.vector.tensor_tensor(
+                out=x_t[r][:, g2],
+                in0=ps["yt", r, g2][:].rearrange("p t c -> p c t"),
+                in1=factor[:, 4 * g2 : 4 * g2 + 4].unsqueeze(1).to_broadcast([P, P, 4]),
+                op=ALU.mult,
+            )
+
+        def y_out(h, c, engine):
+            scaled(engine, x_planes[:, c // 4, c % 4, :], ps["y", h, c][:], factor[:, c : c + 1])
+
+        def interleave(r, engine):
             cols = slice((r % 4) * P, (r % 4 + 1) * P)
             copy(
                 engine,
-                x_t[r // 4][:, g, cols, :].rearrange("p (c i) t -> p c t i", i=4),
-                x_planes[r // 4][:, g, :, cols].rearrange("p t (c i) -> p c t i", i=4),
+                x_t[r][:].rearrange("p g (c i) t -> p g c t i", i=4),
+                x_planes[:, :, :, cols].rearrange("p g t (c i) -> p g c t i", i=4),
             )
 
-        def quantise_x(r, g):
-            cols = slice((r % 4) * P, (r % 4 + 1) * P)
+        def quantise_x(r):
             nc.vector.quantize_mx(
-                out=codes[4 + r // 4][:, g, cols].bitcast(FP8X4), scales=scales[4 + r // 4][:, g, cols],
-                in_=x_t[r // 4][:, g, cols, :].rearrange("p c t -> p (c t)"),
+                out=x_codes[r][:].rearrange("p g c -> p (g c)").bitcast(FP8X4),
+                scales=x_scales[r][:].rearrange("p g c -> p (g c)"),
+                in_=x_t[r][:].rearrange("p g c t -> p (g c t)"),
             )
 
         def stage2(r, th, index):
             ps["out", r, th] = bank(index, "o%d_%d" % (r, th), [P, HALF], F32)
-            cols = slice((r % 4) * P, (r % 4 + 1) * P)
             for g in range(2):
                 nc.tensor.matmul_mx(
                     out=ps["out", r, th][:],
-                    lhsT=codes[4 + r // 4][:, g, cols].bitcast(FP8X4),
-                    lhsT_scale=scales[4 + r // 4][:, g, cols],
+                    lhsT=x_codes[r][:, g, :].bitcast(FP8X4),
+                    lhsT_scale=x_scales[r][:, g, :],
                     rhs=codes[2 + th][:, g, :].bitcast(FP8X4),
                     rhs_scale=scales[2 + th][:, g, :],
                     start=(g == 0),
@@ -356,7 +403,8 @@ def tile_quadraticinverseshrinkagesignalpnl_d2p_kernel(
             "feat": features, "feato": features_out, "total": total, "spread": spread, "widen": widen, "turn": turn,
             "turno": turn_out, "quant": quantise, "pw": permute_words, "psc": permute_scales, "dist": distance,
             "root": inv_root, "eta": eta_pass, "theta": theta_pass, "fin": finish, "s1": stage1, "yo": y_out,
-            "il": interleave, "qx": quantise_x, "s2": stage2, "res": result_out,
+            "il": interleave, "qx": quantise_x, "s1t": stage1_tile, "yd": y_direct, "sigo": signals_out,
+            "ktab": scale_table, "rg": regroup, "s2": stage2, "res": result_out,
         }
         for word in ORDER.split():
             parts = word.split(",")

@@ -24,23 +24,24 @@ H = (CONC**2) ** 0.35 * float(N) ** (-0.35)
 FLOPS = 2 * 2 * N * N * N
 
 ORDER = """
-widen,0,S widen,1,V feat,0,0 feat,1,1 feato,1,S feat,2,2 widen,2,S widen,3,V widen,4,G ktab feat,3,3 feato,3,S
-feato,0,V feato,2,V dist,0,0,4 dist,0,1,5 psc,1,V root,0,0 turn,0,0,6 pw,1,V root,0,1 turn,0,1,7 spread,1
-eta,0,S sigo,0,0 widen,5,G dist,1,0,0 dist,1,1,2 sigo,0,1 turn,1,0,3 root,1,0 theta,0 dist,2,0,4 root,1,1
-widen,6,G turn,1,1,5 eta,1,S turn,2,0,6 sigo,1,0 dist,2,1,7 psc,0,G sigo,1,1 dist,3,0,0 root,2,0 turn,2,1,2
-sigo,2,0 root,2,1 dist,3,1,3 theta,1 root,3,0 widen,7,G dist,4,0,5 dist,4,1,4 root,3,1 dist,5,0,6 dist,5,1,7
-sigo,2,1 root,4,0 quant,0 turn,3,0,0 eta,2,S turn,3,1,3 sigo,3,0 rg,0,G root,4,1 theta,2 root,5,0 eta,3,V
-eta,4,S turn,4,0,2 root,5,1 dist,6,0,5 pw,0,G sigo,3,1 turno,4,0,S total,0,0 eta,5,S theta,3 dist,6,1,4
-dist,7,0,6 turn,4,1,7 theta,4 root,6,0 dist,7,1,2 root,6,1 quant,1 s1t,0,0,3 root,7,0 root,7,1 eta,6,S fin,0
-rg,1,V s1,1,0,5 s1t,0,1,4 rg,2,G theta,5 eta,7,S turn,5,0,6 s1t,1,0,2 theta,6 turno,4,1,S rg,3,G turn,5,1,0
-turno,5,0,S theta,7 turn,6,0,7 turno,5,1,S turn,6,1,6 turno,6,0,S fin,3 turn,7,0,0 fin,5 turno,6,1,S fin,1
-turn,7,1,1 fin,4 fin,6 fin,2 turno,7,0,S fin,7 s1t,1,1,7 fin,8 fin,9 turno,7,1,S fin,10 quant,2 s1,1,1,6
-total,1,0 s1t,2,0,1 fin,11 s1,1,2,0 yd,0,0 yo,1,0,S yo,1,1,S s1,1,3,5 yd,0,1 yo,1,2,S s1,1,4,3 yd,1,0 yo,1,3,S
-s1,1,5,6 quant,3 yo,1,4,S s1,1,6,4 s1,1,7,0 yo,1,5,S yo,1,6,V s1t,2,1,2 yo,1,7,S qx,0 yd,1,1 s1t,3,0,5 il,4,S
-il,5,G yd,2,0 s2,0,1,3 yd,2,1 s2,0,0,6 s1t,3,1,4 qx,1 res,0,0,S qx,2 s2,1,1,0 il,6,G yd,3,0 res,0,1,S s2,1,0,7
-yd,3,1 res,1,1,S s2,2,0,1 res,1,0,S s2,2,1,2 qx,3 res,2,0,V s2,3,1,6 res,2,1,S qx,4 s2,3,0,3 qx,5 res,3,1,S
-qx,6 s2,4,0,5 il,7,V s2,5,0,4 res,3,0,S res,4,0,S res,5,0,V s2,4,1,0 s2,5,1,7 res,4,1,S qx,7 s2,6,1,1
-res,5,1,S s2,7,1,2 res,6,1,V s2,6,0,6 res,7,1,S s2,7,0,3 res,6,0,S res,7,0,V
+widen,0,S widen,1,V feat,0,0 feat,1,1 widen,2,V feat,2,2 feato,0,S ktab feat,3,3 feato,1,V dist,0,0,4
+widen,3,V widen,4,S psc,1,V feato,2,S feato,3,S dist,0,1,5 turn,0,0,6 root,0,0 pw,0,V dist,1,0,7 root,0,1
+dist,1,1,0 root,1,0 dist,2,0,1 turn,0,1,2 turn,1,0,3 widen,5,V root,1,1 psc,0,V eta,0,S widen,6,V dist,2,1,4
+dist,3,0,5 sigo,0,0 root,2,0 root,2,1 turn,1,1,7 sigo,0,1 turn,2,0,0 widen,7,V spread,6 eta,1,S sigo,1,0
+turn,2,1,1 sigo,1,1 root,3,0 turn,3,0,2 sigo,2,0 dist,3,1,4 eta,2,S dist,4,0,3 quant,0 dist,4,1,7 total,0,5
+turn,3,1,0 sigo,2,1 root,3,1 turn,4,0,4 root,4,0 turn,4,1,1 root,4,1 pw,1,V fin,0 turn,5,0,3 dist,5,0,7
+sigo,3,0 dist,5,1,5 eta,3,S eta,4,S root,5,0 theta,0 theta,1 dist,6,0,2 root,5,1 s1,0,0,7 turno,4,0,S
+dist,6,1,5 theta,2 eta,5,S dist,7,0,4 turno,4,1,V root,6,0 s1,0,1,1 root,6,1 dist,7,1,2 root,7,0 eta,6,S
+turn,5,1,5 turn,6,0,4 theta,3 theta,4 theta,5 root,7,1 s1,0,2,2 theta,6 eta,7,S turno,5,0,S theta,7
+turno,5,1,S s1,0,3,3 turn,6,1,5 fin,1 fin,5 fin,3 turn,7,0,6 fin,2 turno,6,0,S turno,6,1,S fin,6 fin,4 fin,7
+turn,7,1,4 fin,9 fin,8 turno,7,0,S quant,2 s1,0,4,5 turno,7,1,S fin,10 sigo,3,1 total,1,6 s1,0,5,4 fin,11
+yo,0,0,S quant,1 s1,0,6,0 s1,0,7,6 yo,0,1,V s1,1,0,7 s1,1,1,1 yo,0,2,V yo,0,3,S yo,0,4,S yo,0,5,S s1,1,2,3
+quant,3 yo,0,6,S s1,1,3,5 yo,0,7,S s1,1,4,2 s1,1,5,4 yo,1,0,S yo,1,1,V il,0,V s1,1,6,0 yo,1,2,S s1,1,7,6
+il,1,V yo,1,3,S qx,0 yo,1,4,S qx,1 s2,0,0,1 il,2,V yo,1,5,S s2,0,1,7 yo,1,6,S s2,1,0,3 qx,2 res,0,0,S
+res,0,1,V s2,2,0,5 yo,1,7,S il,3,V il,4,V s2,1,1,2 s2,2,1,4 res,1,0,S res,2,0,S qx,3 res,1,1,S qx,4 s2,3,1,0
+il,5,V res,2,1,S s2,4,1,1 res,3,1,S s2,3,0,7 qx,5 il,6,V res,4,1,S res,3,0,S il,7,V s2,4,0,6 s2,5,0,3
+res,4,0,S s2,5,1,5 qx,6 res,5,0,V s2,6,1,2 res,5,1,S qx,7 s2,6,0,4 res,6,1,V s2,7,0,0 res,6,0,S s2,7,1,1
+res,7,0,S res,7,1,V
 """
 
 
@@ -154,13 +155,12 @@ def tile_quadraticinverseshrinkagesignalpnl_d2p_kernel(
         sig_t = [sb("sig_t%d" % h, [P, 2, HALF, 4], BF16) for h in range(2)]
         q_t = [sb("q_t%d" % h, [P, 2, HALF, 4], BF16) for h in range(2)]
         x_t = [sb("x_t%d" % r, [P, 2, P, 4], BF16) for r in range(TILES)]
-        x_planes = sb("x_planes", [P, 2, 4, HALF], BF16)
+        x_planes = [sb("x_planes%d" % h, [P, 2, 4, HALF], BF16) for h in range(2)]
         x_codes = [sb("x_codes%d" % r, [P, 2, P], U32) for r in range(TILES)]
         x_scales = [sb("x_scales%d" % r, [P, 2, P], U8) for r in range(TILES)]
         codes = [sb("codes%d" % h, [P, 2, HALF], U32) for h in range(4)]
         scales = [sb("scales%d" % h, [P, 2, HALF], U8) for h in range(4)]
         grouped = sig_t + q_t
-        q_split = [sb("q_split%d" % j, [P, 2, HALF], F32) for j in range(4)]
         k_scale = sb("k_scale", [P, TILES, 2], F32)
         result = [sb("result%d" % r, [P, N], F32) for r in range(TILES)]
         kern = [sb("kern%d" % c, [P, N], F32) for c in range(TILES)]
@@ -214,22 +214,13 @@ def tile_quadraticinverseshrinkagesignalpnl_d2p_kernel(
         def widen(r, engine):
             copy(engine, sig_wide[r][:], sig_bytes[r // 2][:, r % 2, :].bitcast(FP8))
 
-        def regroup(pair, engine):
-            copy(
-                engine,
-                q_split[pair][:].rearrange("p a (g u m) -> p (a g) u m", g=2, u=2),
-                q_rows[pair][:].bitcast(F32).rearrange("p a (g m u) -> p (a g) u m", g=2, u=2),
-            )
-
         def turn(pair, g, index):
             ps["turn", pair, g] = bank(index, "turn%d_%d" % (pair, g), [P, 2, 2, P], F32)
             for a in range(2):
+                rows = sig_wide[2 * pair + a][:] if pair < 4 else q_rows[pair - 4][:, a, :]
+                words = rows.bitcast(F32)
                 for u in range(2):
-                    if pair < 4:
-                        words = sig_wide[2 * pair + a][:].bitcast(F32)[:, 256 * g + u : 256 * (g + 1) : 2]
-                    else:
-                        words = q_split[pair - 4][:, a, (2 * g + u) * P : (2 * g + u + 1) * P]
-                    nc.tensor.transpose(ps["turn", pair, g][:, a, u, :], words, ident32[:])
+                    nc.tensor.transpose(ps["turn", pair, g][:, a, u, :], words[:, 256 * g + u : 256 * (g + 1) : 2], ident32[:])
 
         def turn_out(pair, g, engine):
             dst = grouped[pair // 2][:, g, (pair % 2) * 2 * P : (pair % 2 + 1) * 2 * P, :].bitcast(F32)
@@ -364,14 +355,14 @@ def tile_quadraticinverseshrinkagesignalpnl_d2p_kernel(
             )
 
         def y_out(h, c, engine):
-            scaled(engine, x_planes[:, c // 4, c % 4, :], ps["y", h, c][:], factor[:, c : c + 1])
+            scaled(engine, x_planes[h][:, c // 4, c % 4, :], ps["y", h, c][:], factor[:, c : c + 1])
 
         def interleave(r, engine):
             cols = slice((r % 4) * P, (r % 4 + 1) * P)
             copy(
                 engine,
                 x_t[r][:].rearrange("p g (c i) t -> p g c t i", i=4),
-                x_planes[:, :, :, cols].rearrange("p g t (c i) -> p g c t i", i=4),
+                x_planes[r // 4][:, :, :, cols].rearrange("p g t (c i) -> p g c t i", i=4),
             )
 
         def quantise_x(r):
@@ -404,7 +395,7 @@ def tile_quadraticinverseshrinkagesignalpnl_d2p_kernel(
             "turno": turn_out, "quant": quantise, "pw": permute_words, "psc": permute_scales, "dist": distance,
             "root": inv_root, "eta": eta_pass, "theta": theta_pass, "fin": finish, "s1": stage1, "yo": y_out,
             "il": interleave, "qx": quantise_x, "s1t": stage1_tile, "yd": y_direct, "sigo": signals_out,
-            "ktab": scale_table, "rg": regroup, "s2": stage2, "res": result_out,
+            "ktab": scale_table, "s2": stage2, "res": result_out,
         }
         for word in ORDER.split():
             parts = word.split(",")

@@ -24,24 +24,24 @@ H = (CONC**2) ** 0.35 * float(N) ** (-0.35)
 FLOPS = 2 * 2 * N * N * N
 
 ORDER = """
-widen,0,S widen,1,V feat,0,0 feat,1,1 widen,2,V feat,2,2 feato,0,S ktab feat,3,3 feato,1,V dist,0,0,4
-widen,3,V widen,4,S psc,1,V feato,2,S feato,3,S dist,0,1,5 turn,0,0,6 root,0,0 pw,0,V dist,1,0,7 root,0,1
-dist,1,1,0 root,1,0 dist,2,0,1 turn,0,1,2 turn,1,0,3 widen,5,V root,1,1 psc,0,V eta,0,S widen,6,V dist,2,1,4
-dist,3,0,5 sigo,0,0 root,2,0 root,2,1 turn,1,1,7 sigo,0,1 turn,2,0,0 widen,7,V spread,6 eta,1,S sigo,1,0
-turn,2,1,1 sigo,1,1 root,3,0 turn,3,0,2 sigo,2,0 dist,3,1,4 eta,2,S dist,4,0,3 quant,0 dist,4,1,7 total,0,5
-turn,3,1,0 sigo,2,1 root,3,1 turn,4,0,4 root,4,0 turn,4,1,1 root,4,1 pw,1,V fin,0 turn,5,0,3 dist,5,0,7
-sigo,3,0 dist,5,1,5 eta,3,S eta,4,S root,5,0 theta,0 theta,1 dist,6,0,2 root,5,1 s1,0,0,7 turno,4,0,S
-dist,6,1,5 theta,2 eta,5,S dist,7,0,4 turno,4,1,V root,6,0 s1,0,1,1 root,6,1 dist,7,1,2 root,7,0 eta,6,S
-turn,5,1,5 turn,6,0,4 theta,3 theta,4 theta,5 root,7,1 s1,0,2,2 theta,6 eta,7,S turno,5,0,S theta,7
-turno,5,1,S s1,0,3,3 turn,6,1,5 fin,1 fin,5 fin,3 turn,7,0,6 fin,2 turno,6,0,S turno,6,1,S fin,6 fin,4 fin,7
-turn,7,1,4 fin,9 fin,8 turno,7,0,S quant,2 s1,0,4,5 turno,7,1,S fin,10 sigo,3,1 total,1,6 s1,0,5,4 fin,11
-yo,0,0,S quant,1 s1,0,6,0 s1,0,7,6 yo,0,1,V s1,1,0,7 s1,1,1,1 yo,0,2,V yo,0,3,S yo,0,4,S yo,0,5,S s1,1,2,3
-quant,3 yo,0,6,S s1,1,3,5 yo,0,7,S s1,1,4,2 s1,1,5,4 yo,1,0,S yo,1,1,V il,0,V s1,1,6,0 yo,1,2,S s1,1,7,6
-il,1,V yo,1,3,S qx,0 yo,1,4,S qx,1 s2,0,0,1 il,2,V yo,1,5,S s2,0,1,7 yo,1,6,S s2,1,0,3 qx,2 res,0,0,S
-res,0,1,V s2,2,0,5 yo,1,7,S il,3,V il,4,V s2,1,1,2 s2,2,1,4 res,1,0,S res,2,0,S qx,3 res,1,1,S qx,4 s2,3,1,0
-il,5,V res,2,1,S s2,4,1,1 res,3,1,S s2,3,0,7 qx,5 il,6,V res,4,1,S res,3,0,S il,7,V s2,4,0,6 s2,5,0,3
-res,4,0,S s2,5,1,5 qx,6 res,5,0,V s2,6,1,2 res,5,1,S qx,7 s2,6,0,4 res,6,1,V s2,7,0,0 res,6,0,S s2,7,1,1
-res,7,0,S res,7,1,V
+feat,0,0 widen,0,V widen,1,S feat,1,1 widen,2,V feato,0,S feat,2,2 feato,1,S widen,3,S widen,4,V dist,0,0,3
+feat,3,4 widen,5,V widen,6,V feato,2,S root,0,0 dist,0,1,5 psc,1,V dist,1,0,6 dist,1,1,7 total,0,0 root,0,1 kx
+feato,3,V turn,0,0,1 root,1,0 pw,0,V kt,2 root,1,1 turn,0,1,3 dist,2,0,5 ktab,S eta,0,S sigo,0,0 spread,4
+sigo,0,1 turn,1,0,6 root,2,0 theta,0 dist,2,1,7 eta,1,S dist,3,0,2 turn,1,1,1 widen,7,V turn,2,0,3 root,2,1
+sigo,1,0 dist,3,1,5 root,3,0 dist,4,0,7 sigo,1,1 turn,2,1,6 eta,2,S sigo,2,0 turn,3,0,2 sigo,2,1 root,3,1
+dist,4,1,1 dist,5,0,3 sigo,3,0 root,4,0 dist,5,1,6 dist,6,0,5 dist,6,1,7 eta,3,S pw,1,V dist,7,0,2 root,4,1
+psc,0,V root,5,0 turn,3,1,1 quant,0 root,5,1 root,6,0 turn,4,0,3 root,6,1 theta,1 turn,4,1,6 eta,4,S theta,2
+turn,5,0,5 eta,5,S theta,3 root,7,0 s1,0,0,7 sigo,3,1 turno,4,0,S dist,7,1,2 fin,0 theta,4 eta,6,S turn,5,1,1
+turn,6,0,0 s1,0,1,3 root,7,1 s1,0,2,2 eta,7,S theta,5 theta,6 turno,4,1,S theta,7 turno,5,0,S turn,6,1,6
+turno,5,1,S fin,1 s1,0,3,5 fin,3 fin,5 fin,2 fin,4 turno,6,0,S fin,6 turn,7,0,4 turno,6,1,S fin,7 fin,8 fin,9
+turn,7,1,1 fin,10 quant,1 turno,7,0,S total,1,0 turno,7,1,S fin,11 s1,0,4,6 quant,2 s1,0,5,4 yo,0,0,S yo,0,1,S
+yo,0,2,V yo,0,3,S s1,0,6,1 s1,0,7,0 quant,3 yo,0,4,S s1,1,0,7 yo,0,5,S s1,1,1,3 s1,1,2,2 s1,1,3,5 yo,0,6,V
+yo,0,7,S il,0,V yo,1,0,S il,1,V yo,1,1,S il,2,V yo,1,2,S s1,1,4,6 s1,1,5,4 yo,1,3,S s1,1,6,1 s1,1,7,0 qx,0
+s2,0,1,7 qx,1 qx,2 yo,1,4,S s2,1,1,3 yo,1,5,S yo,1,6,V res,0,1,S il,3,V res,1,1,S st,0,1,2 yo,1,7,V s2,0,0,2
+s2,1,0,5 s2,2,0,6 res,0,0,S st,1,1,2 qx,3 il,4,V res,1,0,S s2,3,0,4 st,0,0,1 res,2,0,S s2,2,1,1 st,1,0,1
+il,5,V res,3,0,S s2,3,1,7 st,2,0,1 qx,4 qx,5 res,2,1,S s2,4,1,3 st,3,0,1 il,6,V res,3,1,S s2,4,0,0 st,2,1,2
+res,4,1,V s2,5,1,2 st,3,1,2 res,4,0,S qx,6 s2,5,0,5 res,5,1,S st,4,0,2 s2,6,0,6 res,5,0,S il,7,V s2,6,1,4
+res,6,0,S st,5,0,2 qx,7 res,6,1,V s2,7,1,1 st,6,0,2 s2,7,0,7 res,7,1,V st,7,1,2 res,7,0,S st,7,0,1
 """
 
 
@@ -83,7 +83,8 @@ def tile_quadraticinverseshrinkagesignalpnl_d2p_kernel(
         warm = sb("warm", [P, 8], F32)
         lam16 = sb("lam16", [P, 2, 4], BF16)
         tilt16 = sb("tilt16", [P, 2, 4], BF16)
-        block_scale = sb("block_scale", [P, TILES * TILES], F32)
+        scale_rows = sb("scale_rows", [P, 4], F32)
+        scale_wide = sb("scale_wide", [P, 4, 32], F32)
         sig_bytes = [sb("sig_bytes%d" % j, [P, 2, N], U8) for j in range(4)]
         q_rows = [sb("q_rows%d" % j, [P, 2, N], BF16) for j in range(4)]
         u_words_raw = sb("u_words_raw", [P, 2, 2 * N], U8)
@@ -100,10 +101,11 @@ def tile_quadraticinverseshrinkagesignalpnl_d2p_kernel(
         sig_view = signals_bytes.rearrange("(r p) k -> p r k", p=P)
         q_view = q.rearrange("(r p) k -> p r k", p=P)
         nc.sync.dma_start(out=lam16[:], in_=lam.rearrange("(g p t) -> p g t", p=P, t=4))
-        nc.sync.dma_start(out=block_scale[:], in_=signals_scale.rearrange("a b -> (a b)").partition_broadcast(P))
         for j in range(4):
             nc.sync.dma_start(out=sig_bytes[j][:], in_=sig_view[:, 2 * j : 2 * j + 2, :])
         nc.vector.memset(warm[:], 1.0)
+        nc.vector.memset(scale_rows[:], 0.0)
+        nc.sync.dma_start(out=scale_rows[0:16, :], in_=signals_scale.rearrange("r (g b) -> (r g) b", g=2))
         nc.vector.memset(u_scales_raw[:].bitcast(I32), 0)
         nc.scalar.activation(out=warm[:, 0:1], in_=warm[:, 1:2], func=ACT.Abs_reciprocal_sqrt)
         nc.sync.dma_start(out=tilt16[:], in_=tilt.rearrange("(g p t) -> p g t", p=P, t=4))
@@ -161,7 +163,7 @@ def tile_quadraticinverseshrinkagesignalpnl_d2p_kernel(
         codes = [sb("codes%d" % h, [P, 2, HALF], U32) for h in range(4)]
         scales = [sb("scales%d" % h, [P, 2, HALF], U8) for h in range(4)]
         grouped = sig_t + q_t
-        k_scale = sb("k_scale", [P, TILES, 2], F32)
+        k_scale = sb("k_scale", [P, 2 * TILES], F32)
         result = [sb("result%d" % r, [P, N], F32) for r in range(TILES)]
         kern = [sb("kern%d" % c, [P, N], F32) for c in range(TILES)]
         eta_sum = small("eta_sum")
@@ -204,12 +206,15 @@ def tile_quadraticinverseshrinkagesignalpnl_d2p_kernel(
                     rhs=rows_j[:, h * HALF : (h + 1) * HALF], start=True, stop=True,
                 )
 
-        def scale_table():
-            for quad in range(4):
-                rows = slice(32 * quad, 32 * quad + 32)
-                nc.vector.tensor_copy(
-                    out=k_scale[rows], in_=block_scale[rows].rearrange("p (r g b) -> p r g b", g=2, b=4)[:, :, :, quad]
-                )
+        def scale_expand():
+            nc.vector.tensor_copy(out=scale_wide[:], in_=scale_rows[:].unsqueeze(2).to_broadcast([P, 4, 32]))
+
+        def scale_turn(index):
+            ps["scale"] = bank(index, "scale_ps", [P, P], F32)
+            nc.tensor.transpose(ps["scale"][:], scale_wide[:].rearrange("p b m -> p (b m)"), ident32[:])
+
+        def scale_table(engine):
+            copy(engine, k_scale[:], ps["scale"][:, 0 : 2 * TILES])
 
         def widen(r, engine):
             copy(engine, sig_wide[r][:], sig_bytes[r // 2][:, r % 2, :].bitcast(FP8))
@@ -231,7 +236,7 @@ def tile_quadraticinverseshrinkagesignalpnl_d2p_kernel(
                 r = 2 * pair + a
                 dst = sig_t[r // 4][:, g, (r % 4) * P : (r % 4 + 1) * P, :].rearrange("p c (u e) -> p c u e", u=2)
                 src = ps["turn", pair, g][:, a].rearrange("p u c -> p (u c)").bitcast(BF16)
-                scaled("V", dst, src.rearrange("p (u c e) -> p c u e", u=2, e=2), k_scale[:, r, g : g + 1])
+                scaled("V", dst, src.rearrange("p (u c e) -> p c u e", u=2, e=2), k_scale[:, 2 * r + g : 2 * r + g + 1])
 
         def quantise(k):
             nc.vector.quantize_mx(
@@ -388,6 +393,9 @@ def tile_quadraticinverseshrinkagesignalpnl_d2p_kernel(
         def result_out(r, th, engine):
             cols = slice(th * HALF, (th + 1) * HALF)
             copy(engine, result[r][:, cols], ps["out", r, th][:])
+
+        def store(r, first, last):
+            cols = slice(first * HALF, last * HALF)
             nc.sync.dma_start(out=out[r * P : (r + 1) * P, cols], in_=result[r][:, cols])
 
         steps = {
@@ -395,7 +403,7 @@ def tile_quadraticinverseshrinkagesignalpnl_d2p_kernel(
             "turno": turn_out, "quant": quantise, "pw": permute_words, "psc": permute_scales, "dist": distance,
             "root": inv_root, "eta": eta_pass, "theta": theta_pass, "fin": finish, "s1": stage1, "yo": y_out,
             "il": interleave, "qx": quantise_x, "s1t": stage1_tile, "yd": y_direct, "sigo": signals_out,
-            "ktab": scale_table, "s2": stage2, "res": result_out,
+            "ktab": scale_table, "kx": scale_expand, "kt": scale_turn, "st": store, "s2": stage2, "res": result_out,
         }
         for word in ORDER.split():
             parts = word.split(",")

@@ -17,32 +17,17 @@ AXIS = mybir.AxisListType
 
 N = 1024
 P = 128
-HALF = 512
 TILES = N // P
+HALF = 512
+QUARTER = 256
+BANKS = 8
 CONC = 0.25
 H = (CONC**2) ** 0.35 * float(N) ** (-0.35)
 FLOPS = 2 * 2 * N * N * N
 
-ORDER = """
-feat,0,0 widen,0,V widen,1,S feat,1,1 widen,2,V feato,0,S feat,2,2 feato,1,S widen,3,S widen,4,V dist,0,0,3
-feat,3,4 widen,5,V widen,6,V feato,2,S root,0,0 dist,0,1,5 psc,1,V dist,1,0,6 dist,1,1,7 total,0,0 root,0,1 kx
-feato,3,V turn,0,0,1 root,1,0 pw,0,V kt,2 root,1,1 turn,0,1,3 dist,2,0,5 ktab,S eta,0,S sigo,0,0 spread,4
-sigo,0,1 turn,1,0,6 root,2,0 theta,0 dist,2,1,7 eta,1,S dist,3,0,2 turn,1,1,1 widen,7,V turn,2,0,3 root,2,1
-sigo,1,0 dist,3,1,5 root,3,0 dist,4,0,7 sigo,1,1 turn,2,1,6 eta,2,S sigo,2,0 turn,3,0,2 sigo,2,1 root,3,1
-dist,4,1,1 dist,5,0,3 sigo,3,0 root,4,0 dist,5,1,6 dist,6,0,5 dist,6,1,7 eta,3,S pw,1,V dist,7,0,2 root,4,1
-psc,0,V root,5,0 turn,3,1,1 quant,0 root,5,1 root,6,0 turn,4,0,3 root,6,1 theta,1 turn,4,1,6 eta,4,S theta,2
-turn,5,0,5 eta,5,S theta,3 root,7,0 s1,0,0,7 sigo,3,1 turno,4,0,S dist,7,1,2 fin,0 theta,4 eta,6,S turn,5,1,1
-turn,6,0,0 s1,0,1,3 root,7,1 s1,0,2,2 eta,7,S theta,5 theta,6 turno,4,1,S theta,7 turno,5,0,S turn,6,1,6
-turno,5,1,S fin,1 s1,0,3,5 fin,3 fin,5 fin,2 fin,4 turno,6,0,S fin,6 turn,7,0,4 turno,6,1,S fin,7 fin,8 fin,9
-turn,7,1,1 fin,10 quant,1 turno,7,0,S total,1,0 turno,7,1,S fin,11 s1,0,4,6 quant,2 s1,0,5,4 yo,0,0,S yo,0,1,S
-yo,0,2,V yo,0,3,S s1,0,6,1 s1,0,7,0 quant,3 yo,0,4,S s1,1,0,7 yo,0,5,S s1,1,1,3 s1,1,2,2 s1,1,3,5 yo,0,6,V
-yo,0,7,S il,0,V yo,1,0,S il,1,V yo,1,1,S il,2,V yo,1,2,S s1,1,4,6 s1,1,5,4 yo,1,3,S s1,1,6,1 s1,1,7,0 qx,0
-s2,0,1,7 qx,1 qx,2 yo,1,4,S s2,1,1,3 yo,1,5,S yo,1,6,V res,0,1,S il,3,V res,1,1,S st,0,1,2 yo,1,7,V s2,0,0,2
-s2,1,0,5 s2,2,0,6 res,0,0,S st,1,1,2 qx,3 il,4,V res,1,0,S s2,3,0,4 st,0,0,1 res,2,0,S s2,2,1,1 st,1,0,1
-il,5,V res,3,0,S s2,3,1,7 st,2,0,1 qx,4 qx,5 res,2,1,S s2,4,1,3 st,3,0,1 il,6,V res,3,1,S s2,4,0,0 st,2,1,2
-res,4,1,V s2,5,1,2 st,3,1,2 res,4,0,S qx,6 s2,5,0,5 res,5,1,S st,4,0,2 s2,6,0,6 res,5,0,S il,7,V s2,6,1,4
-res,6,0,S st,5,0,2 qx,7 res,6,1,V s2,7,1,1 st,6,0,2 s2,7,0,7 res,7,1,V st,7,1,2 res,7,0,S st,7,0,1
-"""
+SCALAR, VECTOR = "scalar", "vector"
+PIECES = ((0, 0, 4), (1, 0, 2), (0, 4, 8), (1, 2, 8))
+Y_ON_VECTOR = ((0, 1), (0, 3), (0, 6), (1, 2), (1, 7))
 
 
 def tile_quadraticinverseshrinkagesignalpnl_d2p_kernel(
@@ -60,22 +45,36 @@ def tile_quadraticinverseshrinkagesignalpnl_d2p_kernel(
         def small(name, width=TILES):
             return sb(name, [P, width], F32)
 
-        def bank(index, name, shape, dtype):
-            return psum.tile(shape, dtype, name=name, tag="bank%d" % index)
+        free_banks = list(range(BANKS))
+        held = {}
+
+        def take(key, shape, dtype):
+            index = free_banks[0]
+            free_banks.remove(index)
+            name = "ps_" + "_".join([str(part) for part in key])
+            held[key] = (index, psum.tile(shape, dtype, name=name, tag="bank%d" % index))
+            return held[key][1]
+
+        def in_psum(key):
+            return held[key][1]
+
+        def give_back(key):
+            free_banks.append(held[key][0])
 
         def copy(engine, dst, src):
-            if engine == "S":
+            if engine == SCALAR:
                 nc.scalar.copy(out=dst, in_=src)
-            elif engine == "G":
-                nc.gpsimd.tensor_copy(out=dst, in_=src)
             else:
                 nc.vector.tensor_copy(out=dst, in_=src)
 
-        def scaled(engine, dst, src, factor):
-            if engine == "S":
-                nc.scalar.activation(out=dst, in_=src, func=ACT.Copy, scale=factor)
+        def scaled(engine, dst, src, per_partition):
+            if engine == SCALAR:
+                nc.scalar.activation(out=dst, in_=src, func=ACT.Copy, scale=per_partition)
             else:
-                nc.vector.tensor_scalar(out=dst, in0=src, scalar1=factor, scalar2=None, op0=ALU.mult)
+                nc.vector.tensor_scalar(out=dst, in0=src, scalar1=per_partition, scalar2=None, op0=ALU.mult)
+
+        def combine(dst, left, right, op):
+            nc.vector.tensor_tensor(out=dst, in0=left, in1=right, op=op)
 
         ident16 = sb("ident16", [P, P], BF16)
         ident32 = sb("ident32", [P, P], F32)
@@ -85,24 +84,24 @@ def tile_quadraticinverseshrinkagesignalpnl_d2p_kernel(
         tilt16 = sb("tilt16", [P, 2, 4], BF16)
         scale_rows = sb("scale_rows", [P, 4], F32)
         scale_wide = sb("scale_wide", [P, 4, 32], F32)
-        sig_bytes = [sb("sig_bytes%d" % j, [P, 2, N], U8) for j in range(4)]
-        q_rows = [sb("q_rows%d" % j, [P, 2, N], BF16) for j in range(4)]
+        sig_bytes = [sb("sig_bytes%d" % pair, [P, 2, N], U8) for pair in range(4)]
+        q_rows = [sb("q_rows%d" % pair, [P, 2, N], BF16) for pair in range(4)]
         u_words_raw = sb("u_words_raw", [P, 2, 2 * N], U8)
         u_scales_raw = sb("u_scales_raw", [P, 2, N], U8)
-        u_w = sb("u_w", [P, 2, 2 * N], U8)
-        u_s = sb("u_s", [P, 2, N], U8)
-        feat_i = sb("feat_i", [P, TILES, P], BF16)
-        feat_j = sb("feat_j", [P, TILES, P], BF16)
-        rows_i = sb("rows_i", [P, N], BF16)
-        rows_j = sb("rows_j", [P, N], BF16)
+        u_words_sliced = sb("u_words_sliced", [P, 2, 2 * N], U8)
+        u_scales_sliced = sb("u_scales_sliced", [P, 2, N], U8)
+        feat_a = sb("feat_a", [P, TILES, P], BF16)
+        feat_b = sb("feat_b", [P, TILES, P], BF16)
+        rows_a = sb("rows_a", [P, N], BF16)
+        rows_b = sb("rows_b", [P, N], BF16)
         lam_flat = lam16[:].rearrange("p g t -> p (g t)")
         tilt_flat = tilt16[:].rearrange("p g t -> p (g t)")
 
         sig_view = signals_bytes.rearrange("(r p) k -> p r k", p=P)
         q_view = q.rearrange("(r p) k -> p r k", p=P)
         nc.sync.dma_start(out=lam16[:], in_=lam.rearrange("(g p t) -> p g t", p=P, t=4))
-        for j in range(4):
-            nc.sync.dma_start(out=sig_bytes[j][:], in_=sig_view[:, 2 * j : 2 * j + 2, :])
+        for pair in range(4):
+            nc.sync.dma_start(out=sig_bytes[pair][:], in_=sig_view[:, 2 * pair : 2 * pair + 2, :])
         nc.vector.memset(warm[:], 1.0)
         nc.vector.memset(scale_rows[:], 0.0)
         nc.sync.dma_start(out=scale_rows[0:16, :], in_=signals_scale.rearrange("r (g b) -> (r g) b", g=2))
@@ -114,39 +113,49 @@ def tile_quadraticinverseshrinkagesignalpnl_d2p_kernel(
                 out=u_scales_raw[32 * quad : 32 * quad + 4].bitcast(I32),
                 in_=u_scales[:, 4 * quad : 4 * quad + 4, :].rearrange("g r n -> r g n").bitcast(I32),
             )
+        for pair in range(2):
+            nc.sync.dma_start(out=q_rows[pair][:], in_=q_view[:, 2 * pair : 2 * pair + 2, :])
         nc.sync.dma_start(out=u_words_raw[:].bitcast(I32), in_=u_words.rearrange("g p n -> p g n").bitcast(I32))
-        for j in range(4):
-            nc.sync.dma_start(out=q_rows[j][:], in_=q_view[:, 2 * j : 2 * j + 2, :])
+        for pair in range(2, 4):
+            nc.sync.dma_start(out=q_rows[pair][:], in_=q_view[:, 2 * pair : 2 * pair + 2, :])
 
         make_identity(nc, ident16[:])
         make_identity(nc, ident32[:])
-        nc.vector.memset(feat_j[:], 0.0)
-        nc.vector.memset(feat_i[:], 0.0)
-        nc.vector.memset(feat_j[:, :, 1:3], 1.0)
-        nc.vector.memset(feat_i[:, :, 3:5], 1.0)
+        nc.vector.memset(feat_b[:], 0.0)
+        nc.vector.memset(feat_a[:], 0.0)
+        nc.vector.memset(feat_b[:, :, 1:3], 1.0)
+        nc.vector.memset(feat_a[:, :, 3:5], 1.0)
         nc.vector.memset(ones32[:], 1.0)
 
+        for g in range(2):
+            nc.gpsimd.tensor_copy(
+                out=u_words_sliced[:, g, :].rearrange("p (h t m b) -> p h t m b", h=2, t=4, b=2),
+                in_=u_words_raw[:, g, :].rearrange("p (h m t b) -> p h t m b", h=2, t=4, b=2),
+            )
+        for g in range(2):
+            nc.gpsimd.tensor_copy(
+                out=u_scales_sliced[:, g, :].rearrange("p (h t m) -> p h t m", h=2, t=4),
+                in_=u_scales_raw[:, g, :].rearrange("p (h m t) -> p h t m", h=2, t=4),
+            )
+
         lam_sq = small("lam_sq")
-        nc.vector.tensor_tensor(out=lam_sq[:], in0=lam_flat, in1=lam_flat, op=ALU.mult)
-        nc.vector.tensor_scalar(out=feat_j[:, :, 0], in0=lam_flat, scalar1=-2.0, scalar2=None, op0=ALU.mult)
-        nc.vector.tensor_copy(out=feat_i[:, :, 0], in_=lam_flat)
-        nc.vector.tensor_copy(out=feat_j[:, :, 3], in_=lam_sq[:])
-        nc.vector.tensor_copy(out=feat_i[:, :, 1], in_=lam_sq[:])
-        nc.vector.tensor_tensor(out=feat_j[:, :, 4], in0=lam_sq[:], in1=feat_j[:, :, 3], op=ALU.subtract)
-        nc.vector.tensor_tensor(out=feat_i[:, :, 2], in0=lam_sq[:], in1=feat_i[:, :, 1], op=ALU.subtract)
+        combine(lam_sq[:], lam_flat, lam_flat, ALU.mult)
+        nc.vector.tensor_scalar(out=feat_b[:, :, 0], in0=lam_flat, scalar1=-2.0, scalar2=None, op0=ALU.mult)
+        nc.vector.tensor_copy(out=feat_a[:, :, 0], in_=lam_flat)
+        nc.vector.tensor_copy(out=feat_b[:, :, 3], in_=lam_sq[:])
+        nc.vector.tensor_copy(out=feat_a[:, :, 1], in_=lam_sq[:])
+        combine(feat_b[:, :, 4], lam_sq[:], feat_b[:, :, 3], ALU.subtract)
+        combine(feat_a[:, :, 2], lam_sq[:], feat_a[:, :, 1], ALU.subtract)
 
         ridge = small("ridge")
         eta_root = small("eta_root")
-        eta_coef = small("eta_coef")
         two_a = small("two_a")
         theta_shift = small("theta_shift")
         two_ha = small("two_ha")
         cube = small("cube")
         lam_part = small("lam_part", 1)
-        root = (CONC * H / N) ** 0.5
         nc.scalar.activation(out=ridge[:], in_=lam_flat, func=ACT.Square, scale=H)
-        nc.scalar.activation(out=eta_root[:], in_=lam_flat, func=ACT.Copy, scale=root)
-        nc.scalar.activation(out=eta_coef[:], in_=lam_flat, func=ACT.Square, scale=root)
+        nc.scalar.activation(out=eta_root[:], in_=lam_flat, func=ACT.Copy, scale=(CONC * H / N) ** 0.5)
         nc.scalar.activation(out=two_a[:], in_=lam_flat, func=ACT.Copy, scale=2.0)
         nc.scalar.activation(out=theta_shift[:], in_=lam_flat, func=ACT.Copy, scale=2.0 * H * (1.0 - CONC))
         nc.scalar.activation(out=two_ha[:], in_=lam_flat, func=ACT.Copy, scale=2.0 * H)
@@ -154,257 +163,320 @@ def tile_quadraticinverseshrinkagesignalpnl_d2p_kernel(
         nc.vector.scalar_tensor_tensor(out=cube[:], in0=ridge[:], scalar=4.0, in1=lam_flat, op0=ALU.mult, op1=ALU.mult)
 
         sig_wide = [sb("sig_wide%d" % r, [P, N], BF16) for r in range(TILES)]
-        sig_t = [sb("sig_t%d" % h, [P, 2, HALF, 4], BF16) for h in range(2)]
-        q_t = [sb("q_t%d" % h, [P, 2, HALF, 4], BF16) for h in range(2)]
-        x_t = [sb("x_t%d" % r, [P, 2, P, 4], BF16) for r in range(TILES)]
-        x_planes = [sb("x_planes%d" % h, [P, 2, 4, HALF], BF16) for h in range(2)]
+        turned = [sb("turned%d" % half, [P, 2, HALF, 4], BF16) for half in range(4)]
+        codes = [sb("codes%d" % half, [P, 2, HALF], U32) for half in range(4)]
+        scales = [sb("scales%d" % half, [P, 2, HALF], U8) for half in range(4)]
+        k_scale = sb("k_scale", [P, 2 * TILES], F32)
+        x_slices = [sb("x_slices%d" % half, [P, 2, 4, HALF], BF16) for half in range(2)]
+        x_grouped = [sb("x_grouped%d" % r, [P, 2, P, 4], BF16) for r in range(TILES)]
         x_codes = [sb("x_codes%d" % r, [P, 2, P], U32) for r in range(TILES)]
         x_scales = [sb("x_scales%d" % r, [P, 2, P], U8) for r in range(TILES)]
-        codes = [sb("codes%d" % h, [P, 2, HALF], U32) for h in range(4)]
-        scales = [sb("scales%d" % h, [P, 2, HALF], U8) for h in range(4)]
-        grouped = sig_t + q_t
-        k_scale = sb("k_scale", [P, 2 * TILES], F32)
         result = [sb("result%d" % r, [P, N], F32) for r in range(TILES)]
         kern = [sb("kern%d" % c, [P, N], F32) for c in range(TILES)]
         eta_sum = small("eta_sum")
         theta_sum = small("theta_sum")
         tilt_coef = small("tilt_coef")
-        eta_sq = small("eta_sq")
-        shifted = small("shifted")
+        eta_term = small("eta_term")
+        theta_term = small("theta_term")
         energy = small("energy")
         inv_energy = small("inv_energy")
         r_values = small("r_values")
         r_part = small("r_part", 1)
         tilted = small("tilted")
         factor = small("factor")
-        ps = {}
 
-        pieces = ((0, 0, 4), (1, 0, 2), (0, 4, 8), (1, 2, 8))
-
-        def features(k, index):
-            side, first, last = pieces[k]
-            ps["feat", k] = bank(index, "feat_ps%d" % k, [P, (last - first) * P], BF16)
-            for c in range(first, last):
+        def features(piece):
+            side, first, end = PIECES[piece]
+            bank = take(("feat", piece), [P, (end - first) * P], BF16)
+            for c in range(first, end):
                 nc.tensor.matmul(
-                    ps["feat", k][:, (c - first) * P : (c - first + 1) * P], lhsT=(feat_j, feat_i)[side][:, c, :],
+                    bank[:, (c - first) * P : (c - first + 1) * P], lhsT=(feat_b, feat_a)[side][:, c, :],
                     rhs=ident16[:], start=True, stop=True,
                 )
 
-        def features_out(k, engine):
-            side, first, last = pieces[k]
-            copy(engine, (rows_j, rows_i)[side][:, first * P : last * P], ps["feat", k][:])
+        def features_out(piece, engine):
+            side, first, end = PIECES[piece]
+            copy(engine, (rows_b, rows_a)[side][:, first * P : end * P], in_psum(("feat", piece))[:])
+            give_back(("feat", piece))
 
-        def total(which, index):
-            ps["total", which] = bank(index, "total%d" % which, [P, 1], F32)
-            nc.tensor.matmul(ps["total", which][:], lhsT=ones32[:], rhs=(lam_part, r_part)[which][:], start=True, stop=True)
+        def total(name, part):
+            nc.tensor.matmul(take((name,), [P, 1], F32)[:], lhsT=ones32[:], rhs=part[:], start=True, stop=True)
 
-        def spread(index):
-            ps["spread"] = bank(index, "minus_2b", [P, N], BF16)
-            for h in range(2):
+        def spread_b():
+            bank = take(("minus_2b",), [P, N], BF16)
+            for half in range(2):
+                cols = slice(half * HALF, (half + 1) * HALF)
                 nc.tensor.matmul(
-                    ps["spread"][:, h * HALF : (h + 1) * HALF], lhsT=ident16[:, 0:1].to_broadcast([P, P]),
-                    rhs=rows_j[:, h * HALF : (h + 1) * HALF], start=True, stop=True,
+                    bank[:, cols], lhsT=ident16[:, 0:1].to_broadcast([P, P]), rhs=rows_b[:, cols], start=True, stop=True
                 )
-
-        def scale_expand():
-            nc.vector.tensor_copy(out=scale_wide[:], in_=scale_rows[:].unsqueeze(2).to_broadcast([P, 4, 32]))
-
-        def scale_turn(index):
-            ps["scale"] = bank(index, "scale_ps", [P, P], F32)
-            nc.tensor.transpose(ps["scale"][:], scale_wide[:].rearrange("p b m -> p (b m)"), ident32[:])
-
-        def scale_table(engine):
-            copy(engine, k_scale[:], ps["scale"][:, 0 : 2 * TILES])
 
         def widen(r, engine):
             copy(engine, sig_wide[r][:], sig_bytes[r // 2][:, r % 2, :].bitcast(FP8))
 
-        def turn(pair, g, index):
-            ps["turn", pair, g] = bank(index, "turn%d_%d" % (pair, g), [P, 2, 2, P], F32)
+        def turn(pair, g):
+            bank = take(("turn", pair, g), [P, 2, 2, P], F32)
             for a in range(2):
                 rows = sig_wide[2 * pair + a][:] if pair < 4 else q_rows[pair - 4][:, a, :]
                 words = rows.bitcast(F32)
                 for u in range(2):
-                    nc.tensor.transpose(ps["turn", pair, g][:, a, u, :], words[:, 256 * g + u : 256 * (g + 1) : 2], ident32[:])
-
-        def turn_out(pair, g, engine):
-            dst = grouped[pair // 2][:, g, (pair % 2) * 2 * P : (pair % 2 + 1) * 2 * P, :].bitcast(F32)
-            copy(engine, dst.rearrange("p (a r) u -> p a r u", a=2), ps["turn", pair, g][:].rearrange("p a u r -> p a r u"))
+                    nc.tensor.transpose(bank[:, a, u, :], words[:, QUARTER * g + u : QUARTER * (g + 1) : 2], ident32[:])
 
         def signals_out(pair, g):
             for a in range(2):
                 r = 2 * pair + a
-                dst = sig_t[r // 4][:, g, (r % 4) * P : (r % 4 + 1) * P, :].rearrange("p c (u e) -> p c u e", u=2)
-                src = ps["turn", pair, g][:, a].rearrange("p u c -> p (u c)").bitcast(BF16)
-                scaled("V", dst, src.rearrange("p (u c e) -> p c u e", u=2, e=2), k_scale[:, 2 * r + g : 2 * r + g + 1])
+                dst = turned[r // 4][:, g, (r % 4) * P : (r % 4 + 1) * P, :].rearrange("p c (u e) -> p c u e", u=2)
+                src = in_psum(("turn", pair, g))[:, a].rearrange("p u c -> p (u c)").bitcast(BF16)
+                scaled(VECTOR, dst, src.rearrange("p (u c e) -> p c u e", u=2, e=2), k_scale[:, 2 * r + g : 2 * r + g + 1])
+            give_back(("turn", pair, g))
 
-        def quantise(k):
+        def q_out(pair, g, engine):
+            dst = turned[pair // 2][:, g, (pair % 2) * QUARTER : (pair % 2 + 1) * QUARTER, :].bitcast(F32)
+            src = in_psum(("turn", pair, g))[:].rearrange("p a u r -> p a r u")
+            copy(engine, dst.rearrange("p (a r) u -> p a r u", a=2), src)
+            give_back(("turn", pair, g))
+
+        def quantise(words, planes, values):
             nc.vector.quantize_mx(
-                out=codes[k][:].rearrange("p g c -> p (g c)").bitcast(FP8X4),
-                scales=scales[k][:].rearrange("p g c -> p (g c)"),
-                in_=grouped[k][:].rearrange("p g c t -> p (g c t)"),
+                out=words[:].rearrange("p g c -> p (g c)").bitcast(FP8X4),
+                scales=planes[:].rearrange("p g c -> p (g c)"),
+                in_=values[:].rearrange("p g c t -> p (g c t)"),
             )
 
-        def permute_words(g, engine):
-            copy(
-                engine,
-                u_w[:, g, :].rearrange("p (h t m b) -> p h t m b", h=2, t=4, b=2),
-                u_words_raw[:, g, :].rearrange("p (h m t b) -> p h t m b", h=2, t=4, b=2),
-            )
+        def quantise_half(half):
+            quantise(codes[half], scales[half], turned[half])
 
-        def permute_scales(g, engine):
-            copy(
-                engine,
-                u_s[:, g, :].rearrange("p (h t m) -> p h t m", h=2, t=4),
-                u_scales_raw[:, g, :].rearrange("p (h m t) -> p h t m", h=2, t=4),
-            )
+        def quantise_x(r):
+            quantise(x_codes[r], x_scales[r], x_grouped[r])
 
-        def distance(c, h, index):
-            ps["dist", c, h] = bank(index, "dist%d_%d" % (c, h), [P, HALF], F32)
+        def distance(c, half):
             nc.tensor.matmul(
-                ps["dist", c, h][:], lhsT=rows_i[:, c * P : (c + 1) * P], rhs=rows_j[:, h * HALF : (h + 1) * HALF],
-                start=True, stop=True,
+                take(("dist", c, half), [P, HALF], F32)[:], lhsT=rows_a[:, c * P : (c + 1) * P],
+                rhs=rows_b[:, half * HALF : (half + 1) * HALF], start=True, stop=True,
             )
 
-        def inv_root(c, h):
+        def inv_root(c, half):
             nc.scalar.activation(
-                out=kern[c][:, h * HALF : (h + 1) * HALF], in_=ps["dist", c, h][:], func=ACT.Abs_reciprocal_sqrt,
-                bias=ridge[:, c : c + 1],
+                out=kern[c][:, half * HALF : (half + 1) * HALF], in_=in_psum(("dist", c, half))[:],
+                func=ACT.Abs_reciprocal_sqrt, bias=ridge[:, c : c + 1],
             )
+            give_back(("dist", c, half))
 
-        def eta_pass(c, engine):
-            if engine == "S":
-                nc.scalar.activation(
-                    out=kern[c][:], in_=kern[c][:], func=ACT.Square, scale=eta_root[:, c : c + 1],
-                    accum_out=eta_sum[:, c : c + 1],
-                )
-            else:
-                nc.vector.scalar_tensor_tensor(
-                    out=kern[c][:], in0=kern[c][:], scalar=eta_coef[:, c : c + 1], in1=kern[c][:],
-                    op0=ALU.mult, op1=ALU.mult, accum_out=eta_sum[:, c : c + 1],
-                )
+        def eta_pass(c):
+            nc.scalar.activation(
+                out=kern[c][:], in_=kern[c][:], func=ACT.Square, scale=eta_root[:, c : c + 1],
+                accum_out=eta_sum[:, c : c + 1],
+            )
 
         def theta_pass(c):
             nc.vector.scalar_tensor_tensor(
-                out=kern[c][:], in0=ps["spread"][:], scalar=two_a[:, c : c + 1], in1=kern[c][:],
+                out=kern[c][:], in0=in_psum(("minus_2b",))[:], scalar=two_a[:, c : c + 1], in1=kern[c][:],
                 op0=ALU.add, op1=ALU.mult, accum_out=theta_sum[:, c : c + 1],
             )
 
-        def product(dst, a, b, op):
-            nc.vector.tensor_tensor(out=dst[:], in0=a, in1=b, op=op)
-
-        def finish(k):
-            if k == 0:
-                scaled("V", tilt_coef[:], cube[:], ps["total", 0][:, 0:1])
-            if k == 1:
-                nc.vector.reciprocal(out=tilt_coef[:], in_=tilt_coef[:])
-            if k == 2:
-                product(tilt_coef, tilt_coef[:], tilt_flat, ALU.mult)
-            if k == 3:
-                product(eta_sq, eta_sum[:], two_ha[:], ALU.mult)
-            if k == 4:
-                product(eta_sq, eta_sq[:], eta_sq[:], ALU.mult)
-            if k == 5:
-                product(shifted, theta_sum[:], theta_shift[:], ALU.add)
-            if k == 6:
-                product(shifted, shifted[:], shifted[:], ALU.mult)
-            if k == 7:
-                product(energy, shifted[:], eta_sq[:], ALU.add)
-            if k == 8:
-                nc.vector.reciprocal(out=inv_energy[:], in_=energy[:])
-            if k == 9:
-                product(tilted, energy[:], tilt_coef[:], ALU.mult)
-            if k == 10:
-                nc.vector.scalar_tensor_tensor(
-                    out=r_values[:], in0=inv_energy[:], scalar=1.0, in1=cube[:], op0=ALU.mult, op1=ALU.mult,
-                    accum_out=r_part[:],
-                )
-            if k == 11:
-                scaled("V", factor[:], tilted[:], ps["total", 1][:, 0:1])
-
-        def stage1(h, c, index):
-            ps["y", h, c] = bank(index, "y%d_%d" % (h, c), [P, HALF], F32)
+        def first_product(half, c):
+            bank = take(("y", half, c), [P, HALF], F32)
             for g in range(2):
                 nc.tensor.matmul_mx(
-                    out=ps["y", h, c][:],
-                    lhsT=u_w[:, g, 2 * P * c : 2 * P * (c + 1)].bitcast(FP4X4),
-                    lhsT_scale=u_s[:, g, P * c : P * (c + 1)],
-                    rhs=codes[h][:, g, :].bitcast(FP8X4),
-                    rhs_scale=scales[h][:, g, :],
+                    out=bank[:],
+                    lhsT=u_words_sliced[:, g, 2 * P * c : 2 * P * (c + 1)].bitcast(FP4X4),
+                    lhsT_scale=u_scales_sliced[:, g, P * c : P * (c + 1)],
+                    rhs=codes[half][:, g, :].bitcast(FP8X4),
+                    rhs_scale=scales[half][:, g, :],
                     start=(g == 0),
                     stop=(g == 1),
                 )
 
-        def stage1_tile(r, g2, index):
-            ps["yt", r, g2] = bank(index, "yt%d_%d" % (r, g2), [P, 4, P], F32)
+        def y_out(half, c):
+            engine = VECTOR if (half, c) in Y_ON_VECTOR else SCALAR
+            scaled(engine, x_slices[half][:, c // 4, c % 4, :], in_psum(("y", half, c))[:], factor[:, c : c + 1])
+            give_back(("y", half, c))
+
+        def interleave(r):
             cols = slice((r % 4) * P, (r % 4 + 1) * P)
-            for t in range(4):
-                c = 4 * g2 + t
-                for g in range(2):
-                    nc.tensor.matmul_mx(
-                        out=ps["yt", r, g2][:, t, :],
-                        lhsT=u_w[:, g, 2 * P * c : 2 * P * (c + 1)].bitcast(FP4X4),
-                        lhsT_scale=u_s[:, g, P * c : P * (c + 1)],
-                        rhs=codes[r // 4][:, g, cols].bitcast(FP8X4),
-                        rhs_scale=scales[r // 4][:, g, cols],
-                        start=(g == 0),
-                        stop=(g == 1),
-                    )
-
-        def y_direct(r, g2):
-            nc.vector.tensor_tensor(
-                out=x_t[r][:, g2],
-                in0=ps["yt", r, g2][:].rearrange("p t c -> p c t"),
-                in1=factor[:, 4 * g2 : 4 * g2 + 4].unsqueeze(1).to_broadcast([P, P, 4]),
-                op=ALU.mult,
+            nc.vector.tensor_copy(
+                out=x_grouped[r][:].rearrange("p g (c i) t -> p g c t i", i=4),
+                in_=x_slices[r // 4][:, :, :, cols].rearrange("p g t (c i) -> p g c t i", i=4),
             )
 
-        def y_out(h, c, engine):
-            scaled(engine, x_planes[h][:, c // 4, c % 4, :], ps["y", h, c][:], factor[:, c : c + 1])
-
-        def interleave(r, engine):
-            cols = slice((r % 4) * P, (r % 4 + 1) * P)
-            copy(
-                engine,
-                x_t[r][:].rearrange("p g (c i) t -> p g c t i", i=4),
-                x_planes[r // 4][:, :, :, cols].rearrange("p g t (c i) -> p g c t i", i=4),
-            )
-
-        def quantise_x(r):
-            nc.vector.quantize_mx(
-                out=x_codes[r][:].rearrange("p g c -> p (g c)").bitcast(FP8X4),
-                scales=x_scales[r][:].rearrange("p g c -> p (g c)"),
-                in_=x_t[r][:].rearrange("p g c t -> p (g c t)"),
-            )
-
-        def stage2(r, th, index):
-            ps["out", r, th] = bank(index, "o%d_%d" % (r, th), [P, HALF], F32)
+        def second_product(r, first, end):
+            width = (end - first) * QUARTER
+            bank = take(("out", r, first), [P, width], F32)
+            cols = slice((first % 2) * QUARTER, (first % 2) * QUARTER + width)
             for g in range(2):
                 nc.tensor.matmul_mx(
-                    out=ps["out", r, th][:],
+                    out=bank[:],
                     lhsT=x_codes[r][:, g, :].bitcast(FP8X4),
                     lhsT_scale=x_scales[r][:, g, :],
-                    rhs=codes[2 + th][:, g, :].bitcast(FP8X4),
-                    rhs_scale=scales[2 + th][:, g, :],
+                    rhs=codes[2 + first // 2][:, g, cols].bitcast(FP8X4),
+                    rhs_scale=scales[2 + first // 2][:, g, cols],
                     start=(g == 0),
                     stop=(g == 1),
                 )
 
-        def result_out(r, th, engine):
-            cols = slice(th * HALF, (th + 1) * HALF)
-            copy(engine, result[r][:, cols], ps["out", r, th][:])
+        def result_out(r, first, end, engine):
+            copy(engine, result[r][:, first * QUARTER : end * QUARTER], in_psum(("out", r, first))[:])
+            give_back(("out", r, first))
 
-        def store(r, first, last):
-            cols = slice(first * HALF, last * HALF)
+        def store(r, first, end):
+            cols = slice(first * QUARTER, end * QUARTER)
             nc.sync.dma_start(out=out[r * P : (r + 1) * P, cols], in_=result[r][:, cols])
 
-        steps = {
-            "feat": features, "feato": features_out, "total": total, "spread": spread, "widen": widen, "turn": turn,
-            "turno": turn_out, "quant": quantise, "pw": permute_words, "psc": permute_scales, "dist": distance,
-            "root": inv_root, "eta": eta_pass, "theta": theta_pass, "fin": finish, "s1": stage1, "yo": y_out,
-            "il": interleave, "qx": quantise_x, "s1t": stage1_tile, "yd": y_direct, "sigo": signals_out,
-            "ktab": scale_table, "kx": scale_expand, "kt": scale_turn, "st": store, "s2": stage2, "res": result_out,
-        }
-        for word in ORDER.split():
-            parts = word.split(",")
-            steps[parts[0]](*[(x if x in "SVG" else int(x)) for x in parts[1:]])
+        widen(1, SCALAR)
+        for piece in range(3):
+            features(piece)
+            features_out(piece, SCALAR)
+        for r in (0, 2, 3, 4):
+            widen(r, VECTOR)
+        nc.vector.tensor_copy(out=scale_wide[:], in_=scale_rows[:].unsqueeze(2).to_broadcast([P, 4, 32]))
+        for r in (5, 6, 7):
+            widen(r, VECTOR)
+        distance(0, 0)
+        distance(0, 1)
+        distance(1, 0)
+        features(3)
+        distance(1, 1)
+        nc.tensor.transpose(take(("scale",), [P, P], F32)[:], scale_wide[:].rearrange("p b m -> p (b m)"), ident32[:])
+        inv_root(0, 0)
+        inv_root(0, 1)
+        features_out(3, VECTOR)
+        nc.vector.tensor_copy(out=k_scale[:], in_=in_psum(("scale",))[:, 0 : 2 * TILES])
+        give_back(("scale",))
+        turn(0, 0)
+        turn(0, 1)
+
+        def distances(c):
+            distance(c, 0)
+            distance(c, 1)
+
+        def scalar_step(c):
+            inv_root(c, 0)
+            inv_root(c, 1)
+            eta_pass(c - 1)
+
+        distances(2)
+        turn(1, 0)
+        scalar_step(1)
+        signals_out(0, 0)
+
+        turn(1, 1)
+        spread_b()
+        distances(3)
+        signals_out(0, 1)
+        scalar_step(2)
+        signals_out(1, 0)
+        signals_out(1, 1)
+        theta_pass(0)
+
+        for c in (3, 4):
+            turn(c - 1, 0)
+            turn(c - 1, 1)
+            distances(c + 1)
+            scalar_step(c)
+            signals_out(2, c - 3)
+            theta_pass(c - 2)
+
+        turn(4, 0)
+        turn(4, 1)
+        signals_out(3, 0)
+        total("lam_total", lam_part)
+        distance(6, 0)
+        inv_root(5, 0)
+        distance(6, 1)
+        inv_root(5, 1)
+        eta_pass(4)
+        theta_pass(3)
+        turn(5, 0)
+        signals_out(3, 1)
+        q_out(4, 0, VECTOR)
+
+        distances(7)
+        scaled(VECTOR, tilt_coef[:], cube[:], in_psum(("lam_total",))[:, 0:1])
+        give_back(("lam_total",))
+        scalar_step(6)
+        turn(5, 1)
+        turn(6, 0)
+        theta_pass(4)
+        nc.vector.reciprocal(out=tilt_coef[:], in_=tilt_coef[:])
+        quantise_half(0)
+        combine(tilt_coef[:], tilt_coef[:], tilt_flat, ALU.mult)
+
+        scalar_step(7)
+        theta_pass(5)
+        quantise_half(1)
+        eta_pass(7)
+        theta_pass(6)
+
+        for c in range(3):
+            first_product(0, c)
+        q_out(4, 1, SCALAR)
+        q_out(5, 0, SCALAR)
+        turn(6, 1)
+        first_product(0, 3)
+        theta_pass(7)
+        give_back(("minus_2b",))
+        q_out(5, 1, SCALAR)
+        turn(7, 0)
+        turn(7, 1)
+        q_out(6, 0, SCALAR)
+        first_product(0, 4)
+        q_out(6, 1, SCALAR)
+        q_out(7, 0, SCALAR)
+        q_out(7, 1, SCALAR)
+        combine(eta_term[:], eta_sum[:], two_ha[:], ALU.mult)
+        combine(theta_term[:], theta_sum[:], theta_shift[:], ALU.add)
+        combine(eta_term[:], eta_term[:], eta_term[:], ALU.mult)
+        combine(theta_term[:], theta_term[:], theta_term[:], ALU.mult)
+        combine(energy[:], theta_term[:], eta_term[:], ALU.add)
+        nc.vector.reciprocal(out=inv_energy[:], in_=energy[:])
+        combine(tilted[:], energy[:], tilt_coef[:], ALU.mult)
+        nc.vector.scalar_tensor_tensor(
+            out=r_values[:], in0=inv_energy[:], scalar=1.0, in1=cube[:], op0=ALU.mult, op1=ALU.mult, accum_out=r_part[:]
+        )
+        total("r_total", r_part)
+        first_product(0, 5)
+        first_product(0, 6)
+        quantise_half(2)
+        scaled(VECTOR, factor[:], tilted[:], in_psum(("r_total",))[:, 0:1])
+        give_back(("r_total",))
+        first_product(0, 7)
+
+        for c in range(TILES):
+            y_out(0, c)
+            first_product(1, c)
+        quantise_half(3)
+        y_out(1, 0)
+        y_out(1, 1)
+        for r in range(3):
+            interleave(r)
+        quantise_x(0)
+        quantise_x(1)
+        y_out(1, 2)
+        quantise_x(2)
+        for c in range(3, TILES):
+            y_out(1, c)
+
+        for r in range(TILES - 1):
+            second_product(r, 0, 2)
+            second_product(r, 2, 4)
+            if r == 0:
+                interleave(3)
+                interleave(4)
+                quantise_x(3)
+                interleave(5)
+                quantise_x(4)
+                quantise_x(5)
+            result_out(r, 0, 2, VECTOR if r in (3, 6) else SCALAR)
+            if r == 0:
+                store(0, 0, 2)
+            if r == 3:
+                interleave(6)
+                interleave(7)
+                quantise_x(6)
+                quantise_x(7)
+            result_out(r, 2, 4, SCALAR)
+            store(r, 2 if r == 0 else 0, 4)
+        last = TILES - 1
+        for first, end, engine in ((0, 2, VECTOR), (2, 3, SCALAR), (3, 4, VECTOR)):
+            second_product(last, first, end)
+            result_out(last, first, end, engine)
+            store(last, first, end)

from contextlib import ExitStack

import concourse.mybir as mybir
from concourse.masks import make_identity

F32 = mybir.dt.float32
BF16 = mybir.dt.bfloat16
U8 = mybir.dt.uint8
U32 = mybir.dt.uint32
I32 = mybir.dt.int32
FP8 = mybir.dt.float8_e4m3fn
FP8X4 = mybir.dt.float8_e4m3fn_x4
FP4X4 = mybir.dt.float4_e2m1fn_x4
ALU = mybir.AluOpType
ACT = mybir.ActivationFunctionType
AXIS = mybir.AxisListType

N = 1024
P = 128
TILES = N // P
HALF = 512
QUARTER = 256
BANKS = 8
CONC = 0.25
H = (CONC**2) ** 0.35 * float(N) ** (-0.35)
FLOPS = 2 * 2 * N * N * N

SCALAR, VECTOR = "scalar", "vector"
PIECES = ((0, 0, 4), (1, 0, 2), (0, 4, 8), (1, 2, 8))
Y_ON_VECTOR = ((0, 1), (0, 3), (0, 6), (1, 2), (1, 7))


def tile_quadraticinverseshrinkagesignalpnl_d2p_kernel(
    tc, signals_bytes, signals_scale, u_words, u_scales, lam, tilt, q, out
):
    nc = tc.nc
    with ExitStack() as ctx:
        keep = ctx.enter_context(tc.tile_pool(name="keep", bufs=1))
        psum = ctx.enter_context(tc.psum_pool(name="psum", bufs=1))
        ctx.enter_context(tc.manual_schedule())

        def sb(name, shape, dtype):
            return keep.tile(shape, dtype, name=name, align_bytes=64)

        def small(name, width=TILES):
            return sb(name, [P, width], F32)

        free_banks = list(range(BANKS))
        held = {}

        def take(key, shape, dtype):
            index = free_banks[0]
            free_banks.remove(index)
            name = "ps_" + "_".join([str(part) for part in key])
            held[key] = (index, psum.tile(shape, dtype, name=name, tag="bank%d" % index))
            return held[key][1]

        def in_psum(key):
            return held[key][1]

        def give_back(key):
            free_banks.append(held[key][0])

        def copy(engine, dst, src):
            if engine == SCALAR:
                nc.scalar.copy(out=dst, in_=src)
            else:
                nc.vector.tensor_copy(out=dst, in_=src)

        def scaled(engine, dst, src, per_partition):
            if engine == SCALAR:
                nc.scalar.activation(out=dst, in_=src, func=ACT.Copy, scale=per_partition)
            else:
                nc.vector.tensor_scalar(out=dst, in0=src, scalar1=per_partition, scalar2=None, op0=ALU.mult)

        def combine(dst, left, right, op):
            nc.vector.tensor_tensor(out=dst, in0=left, in1=right, op=op)

        ident16 = sb("ident16", [P, P], BF16)
        ident32 = sb("ident32", [P, P], F32)
        ones32 = sb("ones32", [P, P], F32)
        warm = sb("warm", [P, 8], F32)
        lam16 = sb("lam16", [P, 2, 4], BF16)
        tilt16 = sb("tilt16", [P, 2, 4], BF16)
        scale_rows = sb("scale_rows", [P, 4], F32)
        scale_wide = sb("scale_wide", [P, 4, 32], F32)
        sig_bytes = [sb("sig_bytes%d" % pair, [P, 2, N], U8) for pair in range(4)]
        q_rows = [sb("q_rows%d" % pair, [P, 2, N], BF16) for pair in range(4)]
        u_words_raw = sb("u_words_raw", [P, 2, 2 * N], U8)
        u_scales_raw = sb("u_scales_raw", [P, 2, N], U8)
        u_words_sliced = sb("u_words_sliced", [P, 2, 2 * N], U8)
        u_scales_sliced = sb("u_scales_sliced", [P, 2, N], U8)
        feat_a = sb("feat_a", [P, TILES, P], BF16)
        feat_b = sb("feat_b", [P, TILES, P], BF16)
        rows_a = sb("rows_a", [P, N], BF16)
        rows_b = sb("rows_b", [P, N], BF16)
        lam_flat = lam16[:].rearrange("p g t -> p (g t)")
        tilt_flat = tilt16[:].rearrange("p g t -> p (g t)")

        sig_view = signals_bytes.rearrange("(r p) k -> p r k", p=P)
        q_view = q.rearrange("(r p) k -> p r k", p=P)
        nc.sync.dma_start(out=lam16[:], in_=lam.rearrange("(g p t) -> p g t", p=P, t=4))
        for pair in range(4):
            nc.sync.dma_start(out=sig_bytes[pair][:], in_=sig_view[:, 2 * pair : 2 * pair + 2, :])
        nc.vector.memset(warm[:], 1.0)
        nc.vector.memset(scale_rows[:], 0.0)
        nc.sync.dma_start(out=scale_rows[0:16, :], in_=signals_scale.rearrange("r (g b) -> (r g) b", g=2))
        nc.vector.memset(u_scales_raw[:].bitcast(I32), 0)
        nc.scalar.activation(out=warm[:, 0:1], in_=warm[:, 1:2], func=ACT.Abs_reciprocal_sqrt)
        nc.sync.dma_start(out=tilt16[:], in_=tilt.rearrange("(g p t) -> p g t", p=P, t=4))
        for quad in range(4):
            nc.sync.dma_start(
                out=u_scales_raw[32 * quad : 32 * quad + 4].bitcast(I32),
                in_=u_scales[:, 4 * quad : 4 * quad + 4, :].rearrange("g r n -> r g n").bitcast(I32),
            )
        for pair in range(2):
            nc.sync.dma_start(out=q_rows[pair][:], in_=q_view[:, 2 * pair : 2 * pair + 2, :])
        nc.sync.dma_start(out=u_words_raw[:].bitcast(I32), in_=u_words.rearrange("g p n -> p g n").bitcast(I32))
        for pair in range(2, 4):
            nc.sync.dma_start(out=q_rows[pair][:], in_=q_view[:, 2 * pair : 2 * pair + 2, :])

        make_identity(nc, ident16[:])
        make_identity(nc, ident32[:])
        nc.vector.memset(feat_b[:], 0.0)
        nc.vector.memset(feat_a[:], 0.0)
        nc.vector.memset(feat_b[:, :, 1:3], 1.0)
        nc.vector.memset(feat_a[:, :, 3:5], 1.0)
        nc.vector.memset(ones32[:], 1.0)

        for g in range(2):
            nc.gpsimd.tensor_copy(
                out=u_words_sliced[:, g, :].rearrange("p (h t m b) -> p h t m b", h=2, t=4, b=2),
                in_=u_words_raw[:, g, :].rearrange("p (h m t b) -> p h t m b", h=2, t=4, b=2),
            )
        for g in range(2):
            nc.gpsimd.tensor_copy(
                out=u_scales_sliced[:, g, :].rearrange("p (h t m) -> p h t m", h=2, t=4),
                in_=u_scales_raw[:, g, :].rearrange("p (h m t) -> p h t m", h=2, t=4),
            )

        lam_sq = small("lam_sq")
        combine(lam_sq[:], lam_flat, lam_flat, ALU.mult)
        nc.vector.tensor_scalar(out=feat_b[:, :, 0], in0=lam_flat, scalar1=-2.0, scalar2=None, op0=ALU.mult)
        nc.vector.tensor_copy(out=feat_a[:, :, 0], in_=lam_flat)
        nc.vector.tensor_copy(out=feat_b[:, :, 3], in_=lam_sq[:])
        nc.vector.tensor_copy(out=feat_a[:, :, 1], in_=lam_sq[:])
        combine(feat_b[:, :, 4], lam_sq[:], feat_b[:, :, 3], ALU.subtract)
        combine(feat_a[:, :, 2], lam_sq[:], feat_a[:, :, 1], ALU.subtract)

        ridge = small("ridge")
        eta_root = small("eta_root")
        two_a = small("two_a")
        theta_shift = small("theta_shift")
        two_ha = small("two_ha")
        cube = small("cube")
        lam_part = small("lam_part", 1)
        nc.scalar.activation(out=ridge[:], in_=lam_flat, func=ACT.Square, scale=H)
        nc.scalar.activation(out=eta_root[:], in_=lam_flat, func=ACT.Copy, scale=(CONC * H / N) ** 0.5)
        nc.scalar.activation(out=two_a[:], in_=lam_flat, func=ACT.Copy, scale=2.0)
        nc.scalar.activation(out=theta_shift[:], in_=lam_flat, func=ACT.Copy, scale=2.0 * H * (1.0 - CONC))
        nc.scalar.activation(out=two_ha[:], in_=lam_flat, func=ACT.Copy, scale=2.0 * H)
        nc.vector.tensor_reduce(out=lam_part[:], in_=lam_flat, axis=AXIS.X, op=ALU.add)
        nc.vector.scalar_tensor_tensor(out=cube[:], in0=ridge[:], scalar=4.0, in1=lam_flat, op0=ALU.mult, op1=ALU.mult)

        sig_wide = [sb("sig_wide%d" % r, [P, N], BF16) for r in range(TILES)]
        turned = [sb("turned%d" % half, [P, 2, HALF, 4], BF16) for half in range(4)]
        codes = [sb("codes%d" % half, [P, 2, HALF], U32) for half in range(4)]
        scales = [sb("scales%d" % half, [P, 2, HALF], U8) for half in range(4)]
        k_scale = sb("k_scale", [P, 2 * TILES], F32)
        x_slices = [sb("x_slices%d" % half, [P, 2, 4, HALF], BF16) for half in range(2)]
        x_grouped = [sb("x_grouped%d" % r, [P, 2, P, 4], BF16) for r in range(TILES)]
        x_codes = [sb("x_codes%d" % r, [P, 2, P], U32) for r in range(TILES)]
        x_scales = [sb("x_scales%d" % r, [P, 2, P], U8) for r in range(TILES)]
        result = [sb("result%d" % r, [P, N], F32) for r in range(TILES)]
        kern = [sb("kern%d" % c, [P, N], F32) for c in range(TILES)]
        eta_sum = small("eta_sum")
        theta_sum = small("theta_sum")
        tilt_coef = small("tilt_coef")
        eta_term = small("eta_term")
        theta_term = small("theta_term")
        energy = small("energy")
        inv_energy = small("inv_energy")
        r_values = small("r_values")
        r_part = small("r_part", 1)
        tilted = small("tilted")
        factor = small("factor")

        def features(piece):
            side, first, end = PIECES[piece]
            bank = take(("feat", piece), [P, (end - first) * P], BF16)
            for c in range(first, end):
                nc.tensor.matmul(
                    bank[:, (c - first) * P : (c - first + 1) * P], lhsT=(feat_b, feat_a)[side][:, c, :],
                    rhs=ident16[:], start=True, stop=True,
                )

        def features_out(piece, engine):
            side, first, end = PIECES[piece]
            copy(engine, (rows_b, rows_a)[side][:, first * P : end * P], in_psum(("feat", piece))[:])
            give_back(("feat", piece))

        def total(name, part):
            nc.tensor.matmul(take((name,), [P, 1], F32)[:], lhsT=ones32[:], rhs=part[:], start=True, stop=True)

        def spread_b():
            bank = take(("minus_2b",), [P, N], BF16)
            for half in range(2):
                cols = slice(half * HALF, (half + 1) * HALF)
                nc.tensor.matmul(
                    bank[:, cols], lhsT=ident16[:, 0:1].to_broadcast([P, P]), rhs=rows_b[:, cols], start=True, stop=True
                )

        def widen(r, engine):
            copy(engine, sig_wide[r][:], sig_bytes[r // 2][:, r % 2, :].bitcast(FP8))

        def turn(pair, g):
            bank = take(("turn", pair, g), [P, 2, 2, P], F32)
            for a in range(2):
                rows = sig_wide[2 * pair + a][:] if pair < 4 else q_rows[pair - 4][:, a, :]
                words = rows.bitcast(F32)
                for u in range(2):
                    nc.tensor.transpose(bank[:, a, u, :], words[:, QUARTER * g + u : QUARTER * (g + 1) : 2], ident32[:])

        def signals_out(pair, g):
            for a in range(2):
                r = 2 * pair + a
                dst = turned[r // 4][:, g, (r % 4) * P : (r % 4 + 1) * P, :].rearrange("p c (u e) -> p c u e", u=2)
                src = in_psum(("turn", pair, g))[:, a].rearrange("p u c -> p (u c)").bitcast(BF16)
                scaled(VECTOR, dst, src.rearrange("p (u c e) -> p c u e", u=2, e=2), k_scale[:, 2 * r + g : 2 * r + g + 1])
            give_back(("turn", pair, g))

        def q_out(pair, g, engine):
            dst = turned[pair // 2][:, g, (pair % 2) * QUARTER : (pair % 2 + 1) * QUARTER, :].bitcast(F32)
            src = in_psum(("turn", pair, g))[:].rearrange("p a u r -> p a r u")
            copy(engine, dst.rearrange("p (a r) u -> p a r u", a=2), src)
            give_back(("turn", pair, g))

        def quantise(words, planes, values):
            nc.vector.quantize_mx(
                out=words[:].rearrange("p g c -> p (g c)").bitcast(FP8X4),
                scales=planes[:].rearrange("p g c -> p (g c)"),
                in_=values[:].rearrange("p g c t -> p (g c t)"),
            )

        def quantise_half(half):
            quantise(codes[half], scales[half], turned[half])

        def quantise_x(r):
            quantise(x_codes[r], x_scales[r], x_grouped[r])

        def distance(c, half):
            nc.tensor.matmul(
                take(("dist", c, half), [P, HALF], F32)[:], lhsT=rows_a[:, c * P : (c + 1) * P],
                rhs=rows_b[:, half * HALF : (half + 1) * HALF], start=True, stop=True,
            )

        def inv_root(c, half):
            nc.scalar.activation(
                out=kern[c][:, half * HALF : (half + 1) * HALF], in_=in_psum(("dist", c, half))[:],
                func=ACT.Abs_reciprocal_sqrt, bias=ridge[:, c : c + 1],
            )
            give_back(("dist", c, half))

        def eta_pass(c):
            nc.scalar.activation(
                out=kern[c][:], in_=kern[c][:], func=ACT.Square, scale=eta_root[:, c : c + 1],
                accum_out=eta_sum[:, c : c + 1],
            )

        def theta_pass(c):
            nc.vector.scalar_tensor_tensor(
                out=kern[c][:], in0=in_psum(("minus_2b",))[:], scalar=two_a[:, c : c + 1], in1=kern[c][:],
                op0=ALU.add, op1=ALU.mult, accum_out=theta_sum[:, c : c + 1],
            )

        def first_product(half, c):
            bank = take(("y", half, c), [P, HALF], F32)
            for g in range(2):
                nc.tensor.matmul_mx(
                    out=bank[:],
                    lhsT=u_words_sliced[:, g, 2 * P * c : 2 * P * (c + 1)].bitcast(FP4X4),
                    lhsT_scale=u_scales_sliced[:, g, P * c : P * (c + 1)],
                    rhs=codes[half][:, g, :].bitcast(FP8X4),
                    rhs_scale=scales[half][:, g, :],
                    start=(g == 0),
                    stop=(g == 1),
                )

        def y_out(half, c):
            engine = VECTOR if (half, c) in Y_ON_VECTOR else SCALAR
            scaled(engine, x_slices[half][:, c // 4, c % 4, :], in_psum(("y", half, c))[:], factor[:, c : c + 1])
            give_back(("y", half, c))

        def interleave(r):
            cols = slice((r % 4) * P, (r % 4 + 1) * P)
            nc.vector.tensor_copy(
                out=x_grouped[r][:].rearrange("p g (c i) t -> p g c t i", i=4),
                in_=x_slices[r // 4][:, :, :, cols].rearrange("p g t (c i) -> p g c t i", i=4),
            )

        def second_product(r, first, end):
            width = (end - first) * QUARTER
            bank = take(("out", r, first), [P, width], F32)
            cols = slice((first % 2) * QUARTER, (first % 2) * QUARTER + width)
            for g in range(2):
                nc.tensor.matmul_mx(
                    out=bank[:],
                    lhsT=x_codes[r][:, g, :].bitcast(FP8X4),
                    lhsT_scale=x_scales[r][:, g, :],
                    rhs=codes[2 + first // 2][:, g, cols].bitcast(FP8X4),
                    rhs_scale=scales[2 + first // 2][:, g, cols],
                    start=(g == 0),
                    stop=(g == 1),
                )

        def result_out(r, first, end, engine):
            copy(engine, result[r][:, first * QUARTER : end * QUARTER], in_psum(("out", r, first))[:])
            give_back(("out", r, first))

        def store(r, first, end):
            cols = slice(first * QUARTER, end * QUARTER)
            nc.sync.dma_start(out=out[r * P : (r + 1) * P, cols], in_=result[r][:, cols])

        widen(1, SCALAR)
        for piece in range(3):
            features(piece)
            features_out(piece, SCALAR)
        for r in (0, 2, 3, 4):
            widen(r, VECTOR)
        nc.vector.tensor_copy(out=scale_wide[:], in_=scale_rows[:].unsqueeze(2).to_broadcast([P, 4, 32]))
        for r in (5, 6, 7):
            widen(r, VECTOR)
        distance(0, 0)
        distance(0, 1)
        distance(1, 0)
        features(3)
        distance(1, 1)
        nc.tensor.transpose(take(("scale",), [P, P], F32)[:], scale_wide[:].rearrange("p b m -> p (b m)"), ident32[:])
        inv_root(0, 0)
        inv_root(0, 1)
        features_out(3, VECTOR)
        nc.vector.tensor_copy(out=k_scale[:], in_=in_psum(("scale",))[:, 0 : 2 * TILES])
        give_back(("scale",))
        turn(0, 0)
        turn(0, 1)

        def distances(c):
            distance(c, 0)
            distance(c, 1)

        def scalar_step(c):
            inv_root(c, 0)
            inv_root(c, 1)
            eta_pass(c - 1)

        distances(2)
        turn(1, 0)
        scalar_step(1)
        signals_out(0, 0)

        turn(1, 1)
        spread_b()
        distances(3)
        signals_out(0, 1)
        scalar_step(2)
        signals_out(1, 0)
        signals_out(1, 1)
        theta_pass(0)

        for c in (3, 4):
            turn(c - 1, 0)
            turn(c - 1, 1)
            distances(c + 1)
            scalar_step(c)
            signals_out(2, c - 3)
            theta_pass(c - 2)

        turn(4, 0)
        turn(4, 1)
        signals_out(3, 0)
        total("lam_total", lam_part)
        distance(6, 0)
        inv_root(5, 0)
        distance(6, 1)
        inv_root(5, 1)
        eta_pass(4)
        theta_pass(3)
        turn(5, 0)
        signals_out(3, 1)
        q_out(4, 0, VECTOR)

        distances(7)
        scaled(VECTOR, tilt_coef[:], cube[:], in_psum(("lam_total",))[:, 0:1])
        give_back(("lam_total",))
        scalar_step(6)
        turn(5, 1)
        turn(6, 0)
        theta_pass(4)
        nc.vector.reciprocal(out=tilt_coef[:], in_=tilt_coef[:])
        quantise_half(0)
        combine(tilt_coef[:], tilt_coef[:], tilt_flat, ALU.mult)

        scalar_step(7)
        theta_pass(5)
        quantise_half(1)
        eta_pass(7)
        theta_pass(6)

        for c in range(3):
            first_product(0, c)
        q_out(4, 1, SCALAR)
        q_out(5, 0, SCALAR)
        turn(6, 1)
        first_product(0, 3)
        theta_pass(7)
        give_back(("minus_2b",))
        q_out(5, 1, SCALAR)
        turn(7, 0)
        turn(7, 1)
        q_out(6, 0, SCALAR)
        first_product(0, 4)
        q_out(6, 1, SCALAR)
        q_out(7, 0, SCALAR)
        q_out(7, 1, SCALAR)
        combine(eta_term[:], eta_sum[:], two_ha[:], ALU.mult)
        combine(theta_term[:], theta_sum[:], theta_shift[:], ALU.add)
        combine(eta_term[:], eta_term[:], eta_term[:], ALU.mult)
        combine(theta_term[:], theta_term[:], theta_term[:], ALU.mult)
        combine(energy[:], theta_term[:], eta_term[:], ALU.add)
        nc.vector.reciprocal(out=inv_energy[:], in_=energy[:])
        combine(tilted[:], energy[:], tilt_coef[:], ALU.mult)
        nc.vector.scalar_tensor_tensor(
            out=r_values[:], in0=inv_energy[:], scalar=1.0, in1=cube[:], op0=ALU.mult, op1=ALU.mult, accum_out=r_part[:]
        )
        total("r_total", r_part)
        first_product(0, 5)
        first_product(0, 6)
        quantise_half(2)
        scaled(VECTOR, factor[:], tilted[:], in_psum(("r_total",))[:, 0:1])
        give_back(("r_total",))
        first_product(0, 7)

        for c in range(TILES):
            y_out(0, c)
            first_product(1, c)
        quantise_half(3)
        y_out(1, 0)
        y_out(1, 1)
        for r in range(3):
            interleave(r)
        quantise_x(0)
        quantise_x(1)
        y_out(1, 2)
        quantise_x(2)
        for c in range(3, TILES):
            y_out(1, c)

        for r in range(TILES - 1):
            second_product(r, 0, 2)
            second_product(r, 2, 4)
            if r == 0:
                interleave(3)
                interleave(4)
                quantise_x(3)
                interleave(5)
                quantise_x(4)
                quantise_x(5)
            result_out(r, 0, 2, VECTOR if r in (3, 6) else SCALAR)
            if r == 0:
                store(0, 0, 2)
            if r == 3:
                interleave(6)
                interleave(7)
                quantise_x(6)
                quantise_x(7)
            result_out(r, 2, 4, SCALAR)
            store(r, 2 if r == 0 else 0, 4)
        last = TILES - 1
        for first, end, engine in ((0, 2, VECTOR), (2, 3, SCALAR), (3, 4, VECTOR)):
            second_product(last, first, end)
            result_out(last, first, end, engine)
            store(last, first, end)
